import numpy as np
import ml_dtypes


def mxq(x, axis, fmt="e4m3"):
    dtype, down = {"e4m3": (ml_dtypes.float8_e4m3fn, 7), "e5m2": (ml_dtypes.float8_e5m2, 14)}[fmt]
    v = np.moveaxis(np.asarray(x, np.float32).astype(ml_dtypes.bfloat16).astype(np.float64), axis, -1)
    blocks = v.reshape(v.shape[:-1] + (-1, 32))
    amax = np.abs(blocks).max(-1, keepdims=True)
    byte = np.maximum(np.where(amax > 0, np.frexp(amax)[1] - 1 + 127, 0) - down, 1)
    scale = np.exp2(byte - 127.0)
    codes = (blocks / scale).astype(np.float32).astype(dtype).astype(np.float64)
    return np.moveaxis((codes * scale).reshape(v.shape), -1, axis)


WIDE = False


def mx_kscale(k):
    if not WIDE:
        return np.ones(k)
    levels = np.array([10, -10, 5, -5, 0])
    if k % 512:
        return np.exp2(np.random.permutation(np.resize(levels, k // 32))).repeat(32)
    a = np.empty((k // 512, 16))
    for p in range(k // 512):
        a[p, :8] = np.random.permutation(np.resize(levels, 8))
        for g in range(8):
            far = levels[np.abs(levels - a[p, g]) >= 10]
            a[p, g + 8] = far[np.random.randint(len(far))]
    return np.exp2(a.ravel()).repeat(32)


def f64(x):
    return np.asarray(x).astype(np.float64)


def striped(idx):
    return np.tile(idx.reshape(-1, 16).T, (8, 1)).astype(np.uint16)


def unstriped(offs):
    return offs[:16].T.reshape(-1).astype(np.int64)


def pack_weight(w):
    k, n = w.shape
    w = f64(np.asarray(w, np.float32).astype(ml_dtypes.bfloat16)).reshape(k // 32, 32, n)
    amax = np.abs(w).max(1)
    byte = np.clip(np.where(amax > 0, np.frexp(amax)[1] - 1 + 127 - 7, 1), 1, 254)
    scaled = (w * np.exp2(127.0 - byte)[:, None, :]).reshape(k, n).astype(np.float32)
    words = np.ascontiguousarray(scaled.reshape(k // 512, 128, 4, n).transpose(0, 1, 3, 2)).astype(ml_dtypes.float8_e4m3fn).view(np.uint8)
    return words, np.ascontiguousarray(byte.astype(np.uint8).reshape(k // 512, 16, n))


def unpack_weight(words, scales):
    g, p, n, _ = words.shape
    vals = np.ascontiguousarray(words).view(ml_dtypes.float8_e4m3fn).astype(np.float64) * np.repeat(np.exp2(scales.astype(np.float64) - 127.0), 8, axis=1)[..., None]
    return vals.transpose(0, 1, 3, 2).reshape(g * 512, n)


def gelu(v):
    return 0.5 * v * (1.0 + np.tanh(np.sqrt(2.0 / np.pi) * (v + 0.044715 * v**3)))


K, T, S, H, N = 1024, 1024, 512, 512, 256
P = 2 ** 7


def setup_inputs():
    n = np.random.standard_normal
    s = mx_kscale(K)[:, None]
    u = mx_kscale(H)
    packed_xT = pack_weight(n((K, T)) * s)
    return {
        "x_words": packed_xT[0],
        "x_scales": packed_xT[1],
        "gate": np.tile(np.random.uniform(0.2, 1.0, S), (P, 1)).astype(np.float32),
        "res": n((N, T)).astype(np.float32),
        "w1": (n((K, H)) / np.sqrt(K) / s * u).astype(np.float32),
        "w2": (n((H, N)) / np.sqrt(H) / u[:, None]).astype(np.float32),
        "offs": striped(np.random.permutation(T)[:S]),
    }


def reference(x_words, x_scales, gate, res, w1, w2, offs):
    r = f64(res)[:, unstriped(offs)]
    xq = unpack_weight(x_words, x_scales)[:, unstriped(offs)]
    h = gelu(mxq(f64(w1), 0, "e4m3").T @ xq)
    y = mxq(f64(w2), 0, "e4m3").T @ mxq(h, 0, "e4m3")
    out = f64(res).copy()
    out[:, unstriped(offs)] = r + y * f64(gate)[:1]
    return out

@@ -1,0 +1,179 @@
+from contextlib import ExitStack
+
+import concourse.mybir as mybir
+from concourse.masks import make_identity
+
+K, T, S, H, N = 1024, 1024, 512, 512, 256
+FLOPS = 2 * S * (K * H + H * N)
+
+F32 = mybir.dt.float32
+BF16 = mybir.dt.bfloat16
+I32 = mybir.dt.int32
+U32 = mybir.dt.uint32
+U16 = mybir.dt.uint16
+U8 = mybir.dt.uint8
+FP8X4 = mybir.dt.float8_e4m3fn_x4
+ACT = mybir.ActivationFunctionType
+ADD = mybir.AluOpType.add
+
+P = 128
+PACK = 4
+K_PASS = P * PACK
+PASSES = K // K_PASS
+CHUNK = 128
+CHUNKS = S // CHUNK
+BLOCKS = N // P
+LANES = 16
+
+
+def tile_picked_modres_mlpgelu_p_kernel(tc, x_words, x_scales, gate, res, w1, w2, offs, out):
+    nc = tc.nc
+    with ExitStack() as ctx:
+        keep = ctx.enter_context(tc.tile_pool(name="keep", bufs=1))
+        psum = ctx.enter_context(tc.psum_pool(name="psum", bufs=1))
+
+        offsets = keep.tile([P, S // LANES], U16, name="offsets")
+        xw = [keep.tile([P, T], I32, name=f"xw{g}", align_bytes=64) for g in range(PASSES)]
+        xs = keep.tile([P, T], U8, name="xs", align_bytes=64)
+        w1a = keep.tile([P, PACK, H], F32, name="w1a", align_bytes=64)
+        w1b = [keep.tile([P, PACK, H // 2], F32, name=f"w1b{u}", align_bytes=64) for u in range(2)]
+        w2raw = keep.tile([P, PACK, N], F32, name="w2raw", align_bytes=64)
+        window = [keep.tile([P, T], F32, name=f"window{b}", align_bytes=64) for b in range(BLOCKS)]
+        gate_rows = keep.tile([P, CHUNK], F32, name="gate_rows", align_bytes=64)
+        ident = keep.tile([P, P], F32, name="ident", align_bytes=64)
+        warm_in = keep.tile([P, 8], F32, name="warm_in", align_bytes=64)
+        warm_out = keep.tile([P, 8], F32, name="warm_out", align_bytes=64)
+
+        nc.vector.memset(xs[:].bitcast(I32), 0)
+        nc.vector.memset(gate_rows[:], 0.0)
+        nc.vector.memset(warm_in[:], 0.0)
+
+        def words(g):
+            return x_words[g].rearrange("p c r -> p (c r)").bitcast(I32)
+
+        def rows(w, g):
+            return w[g * K_PASS : (g + 1) * K_PASS, :].rearrange("(p j) c -> p j c", j=PACK)
+
+        nc.sync.dma_start(out=xw[0][:], in_=words(0))
+        nc.sync.dma_start(offsets[:], offs)
+        nc.scalar.dma_start(out=gate_rows[0:CHUNKS, :], in_=gate[0].rearrange("(c n) -> c n", n=CHUNK))
+        for q in range(4):
+            nc.scalar.dma_start(
+                out=xs[32 * q : 32 * q + 4 * PASSES, :].bitcast(I32),
+                in_=x_scales[:, 4 * q : 4 * q + 4, :].bitcast(I32),
+            )
+        nc.sync.dma_start(out=w1a[:], in_=rows(w1, 0))
+        nc.sync.dma_start(out=xw[1][:], in_=words(1))
+        for u in range(2):
+            nc.sync.dma_start(out=w1b[u][:], in_=rows(w1, 1)[:, :, u * (H // 2) : (u + 1) * (H // 2)])
+        nc.sync.dma_start(out=w2raw[:], in_=rows(w2, 0))
+        for b in range(BLOCKS):
+            nc.sync.dma_start(out=window[b][:], in_=res[b * P : (b + 1) * P, :])
+
+        nc.scalar.activation(warm_out[:], warm_in[:], ACT.Gelu_apprx_tanh)
+        make_identity(nc, ident[:])
+
+        xg = [keep.tile([P, S], U32, name=f"xg{g}", align_bytes=64) for g in range(PASSES)]
+        xsg = keep.tile([P, S], U8, name="xsg", align_bytes=64)
+        w1g = [keep.tile([P, PACK, P, PACK], BF16, name=f"w1g{g}", align_bytes=64) for g in range(PASSES)]
+        w1c = [keep.tile([P, H], U32, name=f"w1c{g}", align_bytes=64) for g in range(PASSES)]
+        w1s = [keep.tile([P, H], U8, name=f"w1s{g}", align_bytes=64) for g in range(PASSES)]
+        w2g = keep.tile([P, N, PACK], BF16, name="w2g", align_bytes=64)
+        w2c = keep.tile([P, N], U32, name="w2c", align_bytes=64)
+        w2s = keep.tile([P, N], U8, name="w2s", align_bytes=64)
+        gate_cols = keep.tile([P, CHUNKS], F32, name="gate_cols", align_bytes=64)
+        picked = [keep.tile([P, S], F32, name=f"picked{b}", align_bytes=64) for b in range(BLOCKS)]
+        update = keep.tile([P, BLOCKS, S], F32, name="update", align_bytes=64)
+
+        def deal_w1(g, raw, m0, count, scalar_count):
+            def views(a, b):
+                dst = w1g[g][:, :, m0 + a : m0 + b, :].rearrange("p t m j -> p m j t")
+                src = raw[:, :, PACK * a : PACK * b].rearrange("p j (m t) -> p m j t", t=PACK)
+                return dst, src
+
+            nc.scalar.copy(*views(0, scalar_count))
+            nc.vector.tensor_copy(*views(scalar_count, count))
+
+        nc.vector.tensor_copy(xg[0][:], xw[0][:].bitcast(U32).indirect(offsets[:]))
+        nc.vector.tensor_copy(xsg[:], xs[:].indirect(offsets[:]))
+
+        gate_ps = psum.tile([P, P], F32, name="gate_ps", tag="turn1")
+        nc.tensor.transpose(gate_ps[:], gate_rows[:], ident[:])
+        nc.scalar.copy(gate_cols[:], gate_ps[:, 0:CHUNKS])
+
+        deal_w1(0, w1a, 0, P, 64)
+        nc.vector.tensor_copy(xg[1][:], xw[1][:].bitcast(U32).indirect(offsets[:]))
+        nc.vector.quantize_mx(out=w1c[0][:].bitcast(FP8X4), scales=w1s[0][:], in_=w1g[0][:].rearrange("p t m j -> p (t m j)"))
+        deal_w1(1, w1b[0], 0, 64, 32)
+        deal_w1(1, w1b[1], 64, 64, 20)
+        for t in range(PACK):
+            cols = slice(t * P, (t + 1) * P)
+            nc.vector.quantize_mx(out=w1c[1][:, cols].bitcast(FP8X4), scales=w1s[1][:, cols], in_=w1g[1][:, t].rearrange("p m j -> p (m j)"))
+
+        nc.vector.tensor_copy(
+            w2g[:].rearrange("p (c i) j -> p c j i", i=4),
+            w2raw[:].rearrange("p j (c i) -> p c j i", i=4),
+        )
+        nc.vector.quantize_mx(out=w2c[:].bitcast(FP8X4), scales=w2s[:], in_=w2g[:].rearrange("p n j -> p (n j)"))
+
+        hg = [keep.tile([P, CHUNK, PACK], BF16, name=f"hg{c}", align_bytes=64) for c in range(CHUNKS)]
+        hc = [keep.tile([P, CHUNK], U32, name=f"hc{c}", align_bytes=64) for c in range(CHUNKS)]
+        hs = [keep.tile([P, CHUNK], U8, name=f"hs{c}", align_bytes=64) for c in range(CHUNKS)]
+        gated = [keep.tile([P, N], F32, name=f"gated{c}", align_bytes=64) for c in range(CHUNKS)]
+
+        def hidden(c):
+            ent = slice(c * CHUNK, (c + 1) * CHUNK)
+            acc = psum.tile([P, PACK, CHUNK], F32, name=f"hid{c}", tag=f"hid{c}")
+            for t in range(PACK):
+                cols = slice(t * P, (t + 1) * P)
+                for g in range(PASSES):
+                    nc.tensor.matmul_mx(
+                        out=acc[:, t, :],
+                        lhsT=w1c[g][:, cols].bitcast(FP8X4),
+                        lhsT_scale=w1s[g][:, cols],
+                        rhs=xg[g][:, ent].bitcast(FP8X4),
+                        rhs_scale=xsg[4 * g : P, ent],
+                        start=(g == 0),
+                        stop=(g == PASSES - 1),
+                    )
+            nc.scalar.activation(hg[c][:], acc[:].rearrange("p t n -> p n t"), ACT.Gelu_apprx_tanh)
+
+        def second(c):
+            ent = slice(c * CHUNK, (c + 1) * CHUNK)
+            nc.vector.quantize_mx(out=hc[c][:].bitcast(FP8X4), scales=hs[c][:], in_=hg[c][:].rearrange("p n t -> p (n t)"))
+            y = psum.tile([P, N], F32, name=f"y{c}", tag=f"y{c % 2}")
+            nc.tensor.matmul_mx(
+                out=y[:], lhsT=hc[c][:].bitcast(FP8X4), lhsT_scale=hs[c][:], rhs=w2c[:].bitcast(FP8X4), rhs_scale=w2s[:], start=True, stop=True
+            )
+            nc.scalar.activation(gated[c][:], y[:], ACT.Copy, scale=gate_cols[:, c : c + 1])
+            turned = psum.tile([P, BLOCKS, CHUNK], F32, name=f"turn{c}", tag=f"turn{c % 2}")
+            for b in range(BLOCKS):
+                nc.tensor.transpose(turned[:, b, :], gated[c][:, b * P : (b + 1) * P], ident[:])
+            nc.scalar.copy(update[:, :, ent], turned[:])
+
+        def look_up(b):
+            nc.vector.tensor_copy(picked[b][:], window[b][:].indirect(offsets[:]))
+
+        def put(b, c0, c1):
+            ent = slice(c0 * CHUNK, c1 * CHUNK)
+            lists = offsets[:, c0 * CHUNK // LANES : c1 * CHUNK // LANES]
+            nc.vector.tensor_tensor(window[b][:].indirect(lists), update[:, b, ent], picked[b][:, ent], ADD)
+
+        hidden(0)
+        look_up(0)
+        hidden(1)
+        second(0)
+        look_up(1)
+        hidden(2)
+        second(1)
+        hidden(3)
+        put(0, 0, 1)
+        second(2)
+        put(1, 0, 1)
+        second(3)
+        put(0, 1, 2)
+        put(1, 1, 2)
+        put(0, 2, 4)
+        nc.sync.dma_start(out=out[0:P, :], in_=window[0][:])
+        put(1, 2, 4)
+        nc.sync.dma_start(out=out[P : 2 * P, :], in_=window[1][:])

@@ -54,18 +54,18 @@ def tile_picked_modres_mlpgelu_p_kernel(tc, x_words, x_scales, gate, res, w1, w2
         def rows(w, g):
             return w[g * K_PASS : (g + 1) * K_PASS, :].rearrange("(p j) c -> p j c", j=PACK)
 
-        nc.sync.dma_start(out=xw[0][:], in_=words(0))
         nc.sync.dma_start(offsets[:], offs)
-        nc.scalar.dma_start(out=gate_rows[0:CHUNKS, :], in_=gate[0].rearrange("(c n) -> c n", n=CHUNK))
+        nc.sync.dma_start(out=xw[0][:], in_=words(0))
         for q in range(4):
-            nc.scalar.dma_start(
+            nc.sync.dma_start(
                 out=xs[32 * q : 32 * q + 4 * PASSES, :].bitcast(I32),
                 in_=x_scales[:, 4 * q : 4 * q + 4, :].bitcast(I32),
             )
+        nc.sync.dma_start(out=gate_rows[0:CHUNKS, :], in_=gate[0].rearrange("(c n) -> c n", n=CHUNK))
         nc.sync.dma_start(out=w1a[:], in_=rows(w1, 0))
-        nc.sync.dma_start(out=xw[1][:], in_=words(1))
         for u in range(2):
             nc.sync.dma_start(out=w1b[u][:], in_=rows(w1, 1)[:, :, u * (H // 2) : (u + 1) * (H // 2)])
+        nc.sync.dma_start(out=xw[1][:], in_=words(1))
         nc.sync.dma_start(out=w2raw[:], in_=rows(w2, 0))
         for b in range(BLOCKS):
             nc.sync.dma_start(out=window[b][:], in_=res[b * P : (b + 1) * P, :])
@@ -73,53 +73,72 @@ def tile_picked_modres_mlpgelu_p_kernel(tc, x_words, x_scales, gate, res, w1, w2
         nc.scalar.activation(warm_out[:], warm_in[:], ACT.Gelu_apprx_tanh)
         make_identity(nc, ident[:])
 
-        xg = [keep.tile([P, S], U32, name=f"xg{g}", align_bytes=64) for g in range(PASSES)]
+        xg = [keep.tile([P, S], U32, name="xg0", align_bytes=64)]
         xsg = keep.tile([P, S], U8, name="xsg", align_bytes=64)
-        w1g = [keep.tile([P, PACK, P, PACK], BF16, name=f"w1g{g}", align_bytes=64) for g in range(PASSES)]
+        w1g = [keep.tile([P, PACK, P, PACK], BF16, name=f"w1g{g}", tag=f"stage{g}", align_bytes=64) for g in range(PASSES)]
         w1c = [keep.tile([P, H], U32, name=f"w1c{g}", align_bytes=64) for g in range(PASSES)]
         w1s = [keep.tile([P, H], U8, name=f"w1s{g}", align_bytes=64) for g in range(PASSES)]
-        w2g = keep.tile([P, N, PACK], BF16, name="w2g", align_bytes=64)
         w2c = keep.tile([P, N], U32, name="w2c", align_bytes=64)
         w2s = keep.tile([P, N], U8, name="w2s", align_bytes=64)
-        gate_cols = keep.tile([P, CHUNKS], F32, name="gate_cols", align_bytes=64)
-        picked = [keep.tile([P, S], F32, name=f"picked{b}", align_bytes=64) for b in range(BLOCKS)]
-        update = keep.tile([P, BLOCKS, S], F32, name="update", align_bytes=64)
+        gate_first = keep.tile([P, 1], F32, name="gate_first", tag="hidden2", align_bytes=64)
+        gate_rest = keep.tile([P, CHUNKS - 1], F32, name="gate_rest", align_bytes=64)
+        gate_cols = [gate_first[:]] + [gate_rest[:, c : c + 1] for c in range(CHUNKS - 1)]
+        picked = {}
+        update_one = [keep.tile([P, BLOCKS, CHUNK], F32, name=f"update{c}", align_bytes=64) for c in range(2)]
+        update_two = keep.tile([P, BLOCKS, 2 * CHUNK], F32, name="update2", align_bytes=64)
+        update = [update_one[0][:], update_one[1][:], update_two[:, :, 0:CHUNK], update_two[:, :, CHUNK:]]
 
-        def deal_w1(g, raw, m0, count, scalar_count):
-            def views(a, b):
-                dst = w1g[g][:, :, m0 + a : m0 + b, :].rearrange("p t m j -> p m j t")
-                src = raw[:, :, PACK * a : PACK * b].rearrange("p j (m t) -> p m j t", t=PACK)
-                return dst, src
-
-            nc.scalar.copy(*views(0, scalar_count))
-            nc.vector.tensor_copy(*views(scalar_count, count))
+        def deal_w1(g, raw, m0, count):
+            for engine_copy, ts in ((nc.scalar.copy, slice(0, 2)), (nc.vector.tensor_copy, slice(2, 4))):
+                engine_copy(
+                    w1g[g][:, ts, m0 : m0 + count, :].rearrange("p t m j -> p m j t"),
+                    raw[:].rearrange("p j (m t) -> p m j t", t=PACK)[:, :, :, ts],
+                )
 
         nc.vector.tensor_copy(xg[0][:], xw[0][:].bitcast(U32).indirect(offsets[:]))
         nc.vector.tensor_copy(xsg[:], xs[:].indirect(offsets[:]))
 
         gate_ps = psum.tile([P, P], F32, name="gate_ps", tag="turn1")
         nc.tensor.transpose(gate_ps[:], gate_rows[:], ident[:])
-        nc.scalar.copy(gate_cols[:], gate_ps[:, 0:CHUNKS])
+        nc.scalar.copy(gate_first[:], gate_ps[:, 0:1])
+        nc.scalar.copy(gate_rest[:], gate_ps[:, 1:CHUNKS])
 
-        deal_w1(0, w1a, 0, P, 64)
-        nc.vector.tensor_copy(xg[1][:], xw[1][:].bitcast(U32).indirect(offsets[:]))
+        deal_w1(0, w1a, 0, P)
+        deal_w1(1, w1b[0], 0, 64)
         nc.vector.quantize_mx(out=w1c[0][:].bitcast(FP8X4), scales=w1s[0][:], in_=w1g[0][:].rearrange("p t m j -> p (t m j)"))
-        deal_w1(1, w1b[0], 0, 64, 32)
-        deal_w1(1, w1b[1], 64, 64, 20)
-        for t in range(PACK):
-            cols = slice(t * P, (t + 1) * P)
-            nc.vector.quantize_mx(out=w1c[1][:, cols].bitcast(FP8X4), scales=w1s[1][:, cols], in_=w1g[1][:, t].rearrange("p m j -> p (m j)"))
+        warm = psum.tile([P, S], F32, name="warm", tag="y1")
+        for width in (S, S, CHUNK):
+            nc.tensor.matmul_mx(
+                out=warm[:, 0:width],
+                lhsT=w1c[0][:, 0:P].bitcast(FP8X4),
+                lhsT_scale=w1s[0][:, 0:P],
+                rhs=xg[0][:, 0:width].bitcast(FP8X4),
+                rhs_scale=xsg[:, 0:width],
+                start=True,
+                stop=True,
+            )
+        deal_w1(1, w1b[1], 64, 64)
+        for t0 in (2, 0):
+            cols = slice(t0 * P, (t0 + 2) * P)
+            nc.vector.quantize_mx(
+                out=w1c[1][:, cols].bitcast(FP8X4), scales=w1s[1][:, cols], in_=w1g[1][:, t0 : t0 + 2].rearrange("p t m j -> p (t m j)")
+            )
+        xg.append(keep.tile([P, S], U32, name="xg1", tag="stage1", align_bytes=64))
+        for c0, c1 in ((0, 1), (1, 2), (2, 4)):
+            lists = offsets[:, c0 * CHUNK // LANES : c1 * CHUNK // LANES]
+            nc.vector.tensor_copy(xg[1][:, c0 * CHUNK : c1 * CHUNK], xw[1][:].bitcast(U32).indirect(lists))
 
+        w2g = keep.tile([P, N, PACK], BF16, name="w2g", align_bytes=64)
         nc.vector.tensor_copy(
             w2g[:].rearrange("p (c i) j -> p c j i", i=4),
             w2raw[:].rearrange("p j (c i) -> p c j i", i=4),
         )
         nc.vector.quantize_mx(out=w2c[:].bitcast(FP8X4), scales=w2s[:], in_=w2g[:].rearrange("p n j -> p (n j)"))
 
-        hg = [keep.tile([P, CHUNK, PACK], BF16, name=f"hg{c}", align_bytes=64) for c in range(CHUNKS)]
+        hg = {}
         hc = [keep.tile([P, CHUNK], U32, name=f"hc{c}", align_bytes=64) for c in range(CHUNKS)]
         hs = [keep.tile([P, CHUNK], U8, name=f"hs{c}", align_bytes=64) for c in range(CHUNKS)]
-        gated = [keep.tile([P, N], F32, name=f"gated{c}", align_bytes=64) for c in range(CHUNKS)]
+        gated = {}
 
         def hidden(c):
             ent = slice(c * CHUNK, (c + 1) * CHUNK)
@@ -136,6 +155,7 @@ def tile_picked_modres_mlpgelu_p_kernel(tc, x_words, x_scales, gate, res, w1, w2
                         start=(g == 0),
                         stop=(g == PASSES - 1),
                     )
+            hg[c] = keep.tile([P, CHUNK, PACK], BF16, name=f"hg{c}", tag=f"hidden{c}", align_bytes=64)
             nc.scalar.activation(hg[c][:], acc[:].rearrange("p t n -> p n t"), ACT.Gelu_apprx_tanh)
 
         def second(c):
@@ -145,32 +165,34 @@ def tile_picked_modres_mlpgelu_p_kernel(tc, x_words, x_scales, gate, res, w1, w2
             nc.tensor.matmul_mx(
                 out=y[:], lhsT=hc[c][:].bitcast(FP8X4), lhsT_scale=hs[c][:], rhs=w2c[:].bitcast(FP8X4), rhs_scale=w2s[:], start=True, stop=True
             )
-            nc.scalar.activation(gated[c][:], y[:], ACT.Copy, scale=gate_cols[:, c : c + 1])
+            gated[c] = keep.tile([P, N], F32, name=f"gated{c}", tag=f"gated{c % 2}", align_bytes=64)
+            nc.scalar.activation(gated[c][:], y[:], ACT.Copy, scale=gate_cols[c])
             turned = psum.tile([P, BLOCKS, CHUNK], F32, name=f"turn{c}", tag=f"turn{c % 2}")
             for b in range(BLOCKS):
                 nc.tensor.transpose(turned[:, b, :], gated[c][:, b * P : (b + 1) * P], ident[:])
-            nc.scalar.copy(update[:, :, ent], turned[:])
+            nc.scalar.copy(update[c], turned[:])
 
         def look_up(b):
+            picked[b] = keep.tile([P, S], F32, name=f"picked{b}", tag=f"hidden{b}", align_bytes=64)
             nc.vector.tensor_copy(picked[b][:], window[b][:].indirect(offsets[:]))
 
         def put(b, c0, c1):
             ent = slice(c0 * CHUNK, c1 * CHUNK)
             lists = offsets[:, c0 * CHUNK // LANES : c1 * CHUNK // LANES]
-            nc.vector.tensor_tensor(window[b][:].indirect(lists), update[:, b, ent], picked[b][:, ent], ADD)
+            nc.vector.tensor_tensor(window[b][:].indirect(lists), (update_one[c0] if c1 - c0 == 1 else update_two)[:, b, :], picked[b][:, ent], ADD)
 
         hidden(0)
-        look_up(0)
         hidden(1)
         second(0)
-        look_up(1)
+        look_up(0)
         hidden(2)
         second(1)
+        look_up(1)
         hidden(3)
-        put(0, 0, 1)
         second(2)
-        put(1, 0, 1)
         second(3)
+        put(0, 0, 1)
+        put(1, 0, 1)
         put(0, 1, 2)
         put(1, 1, 2)
         put(0, 2, 4)

@@ -24,6 +24,7 @@ CHUNK = 128
 CHUNKS = S // CHUNK
 BLOCKS = N // P
 LANES = 16
+HALF = P // 2
 
 
 def tile_picked_modres_mlpgelu_p_kernel(tc, x_words, x_scales, gate, res, w1, w2, offs, out):
@@ -35,8 +36,8 @@ def tile_picked_modres_mlpgelu_p_kernel(tc, x_words, x_scales, gate, res, w1, w2
         offsets = keep.tile([P, S // LANES], U16, name="offsets")
         xw = [keep.tile([P, T], I32, name=f"xw{g}", align_bytes=64) for g in range(PASSES)]
         xs = keep.tile([P, T], U8, name="xs", align_bytes=64)
-        w1a = keep.tile([P, PACK, H], F32, name="w1a", align_bytes=64)
-        w1b = [keep.tile([P, PACK, H // 2], F32, name=f"w1b{u}", align_bytes=64) for u in range(2)]
+        pieces = ((0, 0, P), (1, 0, HALF), (1, HALF, P))
+        w1raw = [keep.tile([P, PACK, PACK * (m1 - m0)], F32, name=f"w1raw{i}", align_bytes=64) for i, (g, m0, m1) in enumerate(pieces)]
         w2raw = keep.tile([P, PACK, N], F32, name="w2raw", align_bytes=64)
         window = [keep.tile([P, T], F32, name=f"window{b}", align_bytes=64) for b in range(BLOCKS)]
         gate_rows = keep.tile([P, CHUNK], F32, name="gate_rows", align_bytes=64)
@@ -62,9 +63,8 @@ def tile_picked_modres_mlpgelu_p_kernel(tc, x_words, x_scales, gate, res, w1, w2
                 in_=x_scales[:, 4 * q : 4 * q + 4, :].bitcast(I32),
             )
         nc.sync.dma_start(out=gate_rows[0:CHUNKS, :], in_=gate[0].rearrange("(c n) -> c n", n=CHUNK))
-        nc.sync.dma_start(out=w1a[:], in_=rows(w1, 0))
-        for u in range(2):
-            nc.sync.dma_start(out=w1b[u][:], in_=rows(w1, 1)[:, :, u * (H // 2) : (u + 1) * (H // 2)])
+        for i, (g, m0, m1) in enumerate(pieces):
+            nc.sync.dma_start(out=w1raw[i][:], in_=rows(w1, g)[:, :, PACK * m0 : PACK * m1])
         nc.sync.dma_start(out=xw[1][:], in_=words(1))
         nc.sync.dma_start(out=w2raw[:], in_=rows(w2, 0))
         for b in range(BLOCKS):
@@ -75,10 +75,9 @@ def tile_picked_modres_mlpgelu_p_kernel(tc, x_words, x_scales, gate, res, w1, w2
 
         xg = [keep.tile([P, S], U32, name="xg0", align_bytes=64)]
         xsg = keep.tile([P, S], U8, name="xsg", align_bytes=64)
-        w1g = [keep.tile([P, PACK, P, PACK], BF16, name=f"w1g{g}", tag=f"stage{g}", align_bytes=64) for g in range(PASSES)]
+        w1g = [keep.tile([P, PACK, P, PACK], BF16, name=f"w1g{g}", align_bytes=64) for g in range(PASSES)]
         w1c = [keep.tile([P, H], U32, name=f"w1c{g}", align_bytes=64) for g in range(PASSES)]
         w1s = [keep.tile([P, H], U8, name=f"w1s{g}", align_bytes=64) for g in range(PASSES)]
-        w2c = keep.tile([P, N], U32, name="w2c", align_bytes=64)
         w2s = keep.tile([P, N], U8, name="w2s", align_bytes=64)
         gate_first = keep.tile([P, 1], F32, name="gate_first", tag="hidden2", align_bytes=64)
         gate_rest = keep.tile([P, CHUNKS - 1], F32, name="gate_rest", align_bytes=64)
@@ -88,11 +87,31 @@ def tile_picked_modres_mlpgelu_p_kernel(tc, x_words, x_scales, gate, res, w1, w2
         update_two = keep.tile([P, BLOCKS, 2 * CHUNK], F32, name="update2", align_bytes=64)
         update = [update_one[0][:], update_one[1][:], update_two[:, :, 0:CHUNK], update_two[:, :, CHUNK:]]
 
-        def deal_w1(g, raw, m0, count):
-            for engine_copy, ts in ((nc.scalar.copy, slice(0, 2)), (nc.vector.tensor_copy, slice(2, 4))):
+        def deal_w1(i, on_scalar):
+            g, m0, m1 = pieces[i]
+            for engine_copy, a, b in ((nc.scalar.copy, 0, on_scalar), (nc.vector.tensor_copy, on_scalar, m1 - m0)):
                 engine_copy(
-                    w1g[g][:, ts, m0 : m0 + count, :].rearrange("p t m j -> p m j t"),
-                    raw[:].rearrange("p j (m t) -> p m j t", t=PACK)[:, :, :, ts],
+                    w1g[g][:, :, m0 + a : m0 + b, :].rearrange("p t m j -> p m j t"),
+                    w1raw[i][:].rearrange("p j (m t) -> p m j t", t=PACK)[:, a:b],
+                )
+
+        def quantise_w1(g):
+            nc.vector.quantize_mx(out=w1c[g][:].bitcast(FP8X4), scales=w1s[g][:], in_=w1g[g][:].rearrange("p t m j -> p (t m j)"))
+
+        acc = [psum.tile([P, PACK, CHUNK], F32, name=f"hid{c}", tag=f"hid{c}") for c in range(CHUNKS)]
+
+        def first_product(c, g):
+            ent = slice(c * CHUNK, (c + 1) * CHUNK)
+            for t in range(PACK):
+                cols = slice(t * P, (t + 1) * P)
+                nc.tensor.matmul_mx(
+                    out=acc[c][:, t, :],
+                    lhsT=w1c[g][:, cols].bitcast(FP8X4),
+                    lhsT_scale=w1s[g][:, cols],
+                    rhs=xg[g][:, ent].bitcast(FP8X4),
+                    rhs_scale=xsg[4 * g : P, ent],
+                    start=(g == 0 and t == 0),
+                    stop=(g == PASSES - 1 and t == PACK - 1),
                 )
 
         nc.vector.tensor_copy(xg[0][:], xw[0][:].bitcast(U32).indirect(offsets[:]))
@@ -103,27 +122,14 @@ def tile_picked_modres_mlpgelu_p_kernel(tc, x_words, x_scales, gate, res, w1, w2
         nc.scalar.copy(gate_first[:], gate_ps[:, 0:1])
         nc.scalar.copy(gate_rest[:], gate_ps[:, 1:CHUNKS])
 
-        deal_w1(0, w1a, 0, P)
-        deal_w1(1, w1b[0], 0, 64)
-        nc.vector.quantize_mx(out=w1c[0][:].bitcast(FP8X4), scales=w1s[0][:], in_=w1g[0][:].rearrange("p t m j -> p (t m j)"))
-        warm = psum.tile([P, S], F32, name="warm", tag="y1")
-        for width in (S, S, CHUNK):
-            nc.tensor.matmul_mx(
-                out=warm[:, 0:width],
-                lhsT=w1c[0][:, 0:P].bitcast(FP8X4),
-                lhsT_scale=w1s[0][:, 0:P],
-                rhs=xg[0][:, 0:width].bitcast(FP8X4),
-                rhs_scale=xsg[:, 0:width],
-                start=True,
-                stop=True,
-            )
-        deal_w1(1, w1b[1], 64, 64)
-        for t0 in (2, 0):
-            cols = slice(t0 * P, (t0 + 2) * P)
-            nc.vector.quantize_mx(
-                out=w1c[1][:, cols].bitcast(FP8X4), scales=w1s[1][:, cols], in_=w1g[1][:, t0 : t0 + 2].rearrange("p t m j -> p (t m j)")
-            )
-        xg.append(keep.tile([P, S], U32, name="xg1", tag="stage1", align_bytes=64))
+        deal_w1(0, 48)
+        quantise_w1(0)
+        first_product(0, 0)
+        first_product(1, 0)
+        deal_w1(1, 40)
+        deal_w1(2, 24)
+        quantise_w1(1)
+        xg.append(keep.tile([P, S], U32, name="xg1", align_bytes=64))
         for c0, c1 in ((0, 1), (1, 2), (2, 4)):
             lists = offsets[:, c0 * CHUNK // LANES : c1 * CHUNK // LANES]
             nc.vector.tensor_copy(xg[1][:, c0 * CHUNK : c1 * CHUNK], xw[1][:].bitcast(U32).indirect(lists))
@@ -133,7 +139,6 @@ def tile_picked_modres_mlpgelu_p_kernel(tc, x_words, x_scales, gate, res, w1, w2
             w2g[:].rearrange("p (c i) j -> p c j i", i=4),
             w2raw[:].rearrange("p j (c i) -> p c j i", i=4),
         )
-        nc.vector.quantize_mx(out=w2c[:].bitcast(FP8X4), scales=w2s[:], in_=w2g[:].rearrange("p n j -> p (n j)"))
 
         hg = {}
         hc = [keep.tile([P, CHUNK], U32, name=f"hc{c}", align_bytes=64) for c in range(CHUNKS)]
@@ -141,26 +146,14 @@ def tile_picked_modres_mlpgelu_p_kernel(tc, x_words, x_scales, gate, res, w1, w2
         gated = {}
 
         def hidden(c):
-            ent = slice(c * CHUNK, (c + 1) * CHUNK)
-            acc = psum.tile([P, PACK, CHUNK], F32, name=f"hid{c}", tag=f"hid{c}")
-            for t in range(PACK):
-                cols = slice(t * P, (t + 1) * P)
-                for g in range(PASSES):
-                    nc.tensor.matmul_mx(
-                        out=acc[:, t, :],
-                        lhsT=w1c[g][:, cols].bitcast(FP8X4),
-                        lhsT_scale=w1s[g][:, cols],
-                        rhs=xg[g][:, ent].bitcast(FP8X4),
-                        rhs_scale=xsg[4 * g : P, ent],
-                        start=(g == 0),
-                        stop=(g == PASSES - 1),
-                    )
+            first_product(c, 1)
             hg[c] = keep.tile([P, CHUNK, PACK], BF16, name=f"hg{c}", tag=f"hidden{c}", align_bytes=64)
-            nc.scalar.activation(hg[c][:], acc[:].rearrange("p t n -> p n t"), ACT.Gelu_apprx_tanh)
+            nc.scalar.activation(hg[c][:], acc[c][:].rearrange("p t n -> p n t"), ACT.Gelu_apprx_tanh)
+
+        def quantise_hidden(c):
+            nc.vector.quantize_mx(out=hc[c][:].bitcast(FP8X4), scales=hs[c][:], in_=hg[c][:].rearrange("p n t -> p (n t)"))
 
         def second(c):
-            ent = slice(c * CHUNK, (c + 1) * CHUNK)
-            nc.vector.quantize_mx(out=hc[c][:].bitcast(FP8X4), scales=hs[c][:], in_=hg[c][:].rearrange("p n t -> p (n t)"))
             y = psum.tile([P, N], F32, name=f"y{c}", tag=f"y{c % 2}")
             nc.tensor.matmul_mx(
                 out=y[:], lhsT=hc[c][:].bitcast(FP8X4), lhsT_scale=hs[c][:], rhs=w2c[:].bitcast(FP8X4), rhs_scale=w2s[:], start=True, stop=True
@@ -172,8 +165,8 @@ def tile_picked_modres_mlpgelu_p_kernel(tc, x_words, x_scales, gate, res, w1, w2
                 nc.tensor.transpose(turned[:, b, :], gated[c][:, b * P : (b + 1) * P], ident[:])
             nc.scalar.copy(update[c], turned[:])
 
-        def look_up(b):
-            picked[b] = keep.tile([P, S], F32, name=f"picked{b}", tag=f"hidden{b}", align_bytes=64)
+        def look_up(b, tag):
+            picked[b] = keep.tile([P, S], F32, name=f"picked{b}", tag=tag, align_bytes=64)
             nc.vector.tensor_copy(picked[b][:], window[b][:].indirect(offsets[:]))
 
         def put(b, c0, c1):
@@ -182,14 +175,22 @@ def tile_picked_modres_mlpgelu_p_kernel(tc, x_words, x_scales, gate, res, w1, w2
             nc.vector.tensor_tensor(window[b][:].indirect(lists), (update_one[c0] if c1 - c0 == 1 else update_two)[:, b, :], picked[b][:, ent], ADD)
 
         hidden(0)
+        first_product(2, 0)
         hidden(1)
+        first_product(3, 0)
+        quantise_hidden(0)
+        w2c = keep.tile([P, N], U32, name="w2c", align_bytes=64)
+        nc.vector.quantize_mx(out=w2c[:].bitcast(FP8X4), scales=w2s[:], in_=w2g[:].rearrange("p n j -> p (n j)"))
         second(0)
-        look_up(0)
+        look_up(0, "hidden0")
         hidden(2)
+        quantise_hidden(1)
         second(1)
-        look_up(1)
+        look_up(1, "picked1")
         hidden(3)
+        quantise_hidden(2)
         second(2)
+        quantise_hidden(3)
         second(3)
         put(0, 0, 1)
         put(1, 0, 1)

@@ -45,8 +45,8 @@ def tile_picked_modres_mlpgelu_p_kernel(tc, x_words, x_scales, gate, res, w1, w2
         warm_in = keep.tile([P, 8], F32, name="warm_in", align_bytes=64)
         warm_out = keep.tile([P, 8], F32, name="warm_out", align_bytes=64)
 
-        nc.vector.memset(xs[:].bitcast(I32), 0)
-        nc.vector.memset(gate_rows[:], 0.0)
+        nc.gpsimd.memset(xs[:].bitcast(I32), 0)
+        nc.gpsimd.memset(gate_rows[:], 0.0)
         nc.vector.memset(warm_in[:], 0.0)
 
         def words(g):
@@ -55,8 +55,8 @@ def tile_picked_modres_mlpgelu_p_kernel(tc, x_words, x_scales, gate, res, w1, w2
         def rows(w, g):
             return w[g * K_PASS : (g + 1) * K_PASS, :].rearrange("(p j) c -> p j c", j=PACK)
 
-        nc.sync.dma_start(offsets[:], offs)
         nc.sync.dma_start(out=xw[0][:], in_=words(0))
+        nc.sync.dma_start(offsets[:], offs)
         for q in range(4):
             nc.sync.dma_start(
                 out=xs[32 * q : 32 * q + 4 * PASSES, :].bitcast(I32),

@@ -36,7 +36,7 @@ def tile_picked_modres_mlpgelu_p_kernel(tc, x_words, x_scales, gate, res, w1, w2
         offsets = keep.tile([P, S // LANES], U16, name="offsets")
         xw = [keep.tile([P, T], I32, name=f"xw{g}", align_bytes=64) for g in range(PASSES)]
         xs = keep.tile([P, T], U8, name="xs", align_bytes=64)
-        pieces = ((0, 0, P), (1, 0, HALF), (1, HALF, P))
+        pieces = ((0, 0, P), (1, 0, P))
         w1raw = [keep.tile([P, PACK, PACK * (m1 - m0)], F32, name=f"w1raw{i}", align_bytes=64) for i, (g, m0, m1) in enumerate(pieces)]
         w2raw = keep.tile([P, PACK, N], F32, name="w2raw", align_bytes=64)
         window = [keep.tile([P, T], F32, name=f"window{b}", align_bytes=64) for b in range(BLOCKS)]
@@ -126,8 +126,7 @@ def tile_picked_modres_mlpgelu_p_kernel(tc, x_words, x_scales, gate, res, w1, w2
         quantise_w1(0)
         first_product(0, 0)
         first_product(1, 0)
-        deal_w1(1, 40)
-        deal_w1(2, 24)
+        deal_w1(1, 48)
         quantise_w1(1)
         xg.append(keep.tile([P, S], U32, name="xg1", align_bytes=64))
         for c0, c1 in ((0, 1), (1, 2), (2, 4)):

@@ -102,7 +102,7 @@ def tile_picked_modres_mlpgelu_p_kernel(tc, x_words, x_scales, gate, res, w1, w2
 
         def first_product(c, g):
             ent = slice(c * CHUNK, (c + 1) * CHUNK)
-            for t in range(PACK):
+            for t in reversed(range(PACK)):
                 cols = slice(t * P, (t + 1) * P)
                 nc.tensor.matmul_mx(
                     out=acc[c][:, t, :],
@@ -110,8 +110,8 @@ def tile_picked_modres_mlpgelu_p_kernel(tc, x_words, x_scales, gate, res, w1, w2
                     lhsT_scale=w1s[g][:, cols],
                     rhs=xg[g][:, ent].bitcast(FP8X4),
                     rhs_scale=xsg[4 * g : P, ent],
-                    start=(g == 0 and t == 0),
-                    stop=(g == PASSES - 1 and t == PACK - 1),
+                    start=(g == 0 and t == PACK - 1),
+                    stop=(g == PASSES - 1 and t == 0),
                 )
 
         nc.vector.tensor_copy(xg[0][:], xw[0][:].bitcast(U32).indirect(offsets[:]))
@@ -126,8 +126,14 @@ def tile_picked_modres_mlpgelu_p_kernel(tc, x_words, x_scales, gate, res, w1, w2
         quantise_w1(0)
         first_product(0, 0)
         first_product(1, 0)
-        deal_w1(1, 48)
-        quantise_w1(1)
+        source = w1raw[1][:].rearrange("p j (m t) -> p m j t", t=PACK)
+        for engine_copy, t0, m0, m1 in ((nc.vector.tensor_copy, 2, 0, P), (nc.scalar.copy, 0, 0, 104), (nc.vector.tensor_copy, 0, 104, P)):
+            engine_copy(w1g[1][:, t0 : t0 + 2, m0:m1, :].rearrange("p t m j -> p m j t"), source[:, m0:m1, :, t0 : t0 + 2])
+        for t0 in (2, 0):
+            cols = slice(t0 * P, (t0 + 2) * P)
+            nc.vector.quantize_mx(
+                out=w1c[1][:, cols].bitcast(FP8X4), scales=w1s[1][:, cols], in_=w1g[1][:, t0 : t0 + 2].rearrange("p t m j -> p (t m j)")
+            )
         xg.append(keep.tile([P, S], U32, name="xg1", align_bytes=64))
         for c0, c1 in ((0, 1), (1, 2), (2, 4)):
             lists = offsets[:, c0 * CHUNK // LANES : c1 * CHUNK // LANES]

@@ -87,16 +87,16 @@ def tile_picked_modres_mlpgelu_p_kernel(tc, x_words, x_scales, gate, res, w1, w2
         update_two = keep.tile([P, BLOCKS, 2 * CHUNK], F32, name="update2", align_bytes=64)
         update = [update_one[0][:], update_one[1][:], update_two[:, :, 0:CHUNK], update_two[:, :, CHUNK:]]
 
-        def deal_w1(i, on_scalar):
-            g, m0, m1 = pieces[i]
-            for engine_copy, a, b in ((nc.scalar.copy, 0, on_scalar), (nc.vector.tensor_copy, on_scalar, m1 - m0)):
-                engine_copy(
-                    w1g[g][:, :, m0 + a : m0 + b, :].rearrange("p t m j -> p m j t"),
-                    w1raw[i][:].rearrange("p j (m t) -> p m j t", t=PACK)[:, a:b],
-                )
+        def deal_w1(g):
+            source = w1raw[g][:].rearrange("p j (m t) -> p m j t", t=PACK)
+            for engine_copy, t0 in ((nc.vector.tensor_copy, 2), (nc.scalar.copy, 0)):
+                engine_copy(w1g[g][:, t0 : t0 + 2].rearrange("p t m j -> p m j t"), source[:, :, :, t0 : t0 + 2])
 
-        def quantise_w1(g):
-            nc.vector.quantize_mx(out=w1c[g][:].bitcast(FP8X4), scales=w1s[g][:], in_=w1g[g][:].rearrange("p t m j -> p (t m j)"))
+        def quantise_w1(g, t0):
+            cols = slice(t0 * P, (t0 + 2) * P)
+            nc.vector.quantize_mx(
+                out=w1c[g][:, cols].bitcast(FP8X4), scales=w1s[g][:, cols], in_=w1g[g][:, t0 : t0 + 2].rearrange("p t m j -> p (t m j)")
+            )
 
         acc = [psum.tile([P, PACK, CHUNK], F32, name=f"hid{c}", tag=f"hid{c}") for c in range(CHUNKS)]
 
@@ -122,22 +122,23 @@ def tile_picked_modres_mlpgelu_p_kernel(tc, x_words, x_scales, gate, res, w1, w2
         nc.scalar.copy(gate_first[:], gate_ps[:, 0:1])
         nc.scalar.copy(gate_rest[:], gate_ps[:, 1:CHUNKS])
 
-        deal_w1(0, 48)
-        quantise_w1(0)
-        first_product(0, 0)
-        first_product(1, 0)
-        source = w1raw[1][:].rearrange("p j (m t) -> p m j t", t=PACK)
-        for engine_copy, t0, m0, m1 in ((nc.vector.tensor_copy, 2, 0, P), (nc.scalar.copy, 0, 0, 104), (nc.vector.tensor_copy, 0, 104, P)):
-            engine_copy(w1g[1][:, t0 : t0 + 2, m0:m1, :].rearrange("p t m j -> p m j t"), source[:, m0:m1, :, t0 : t0 + 2])
-        for t0 in (2, 0):
-            cols = slice(t0 * P, (t0 + 2) * P)
-            nc.vector.quantize_mx(
-                out=w1c[1][:, cols].bitcast(FP8X4), scales=w1s[1][:, cols], in_=w1g[1][:, t0 : t0 + 2].rearrange("p t m j -> p (t m j)")
-            )
         xg.append(keep.tile([P, S], U32, name="xg1", align_bytes=64))
-        for c0, c1 in ((0, 1), (1, 2), (2, 4)):
+
+        def gather_second_pass(c0, c1):
             lists = offsets[:, c0 * CHUNK // LANES : c1 * CHUNK // LANES]
             nc.vector.tensor_copy(xg[1][:, c0 * CHUNK : c1 * CHUNK], xw[1][:].bitcast(U32).indirect(lists))
+
+        deal_w1(0)
+        quantise_w1(0, 2)
+        quantise_w1(0, 0)
+        first_product(0, 0)
+        first_product(1, 0)
+        deal_w1(1)
+        quantise_w1(1, 2)
+        gather_second_pass(0, 1)
+        quantise_w1(1, 0)
+        gather_second_pass(1, 2)
+        gather_second_pass(2, 4)
 
         w2g = keep.tile([P, N, PACK], BF16, name="w2g", align_bytes=64)
         nc.vector.tensor_copy(

@@ -79,13 +79,9 @@ def tile_picked_modres_mlpgelu_p_kernel(tc, x_words, x_scales, gate, res, w1, w2
         w1c = [keep.tile([P, H], U32, name=f"w1c{g}", align_bytes=64) for g in range(PASSES)]
         w1s = [keep.tile([P, H], U8, name=f"w1s{g}", align_bytes=64) for g in range(PASSES)]
         w2s = keep.tile([P, N], U8, name="w2s", align_bytes=64)
-        gate_first = keep.tile([P, 1], F32, name="gate_first", tag="hidden2", align_bytes=64)
-        gate_rest = keep.tile([P, CHUNKS - 1], F32, name="gate_rest", align_bytes=64)
-        gate_cols = [gate_first[:]] + [gate_rest[:, c : c + 1] for c in range(CHUNKS - 1)]
+        gate_cols = keep.tile([P, CHUNKS], F32, name="gate_cols", align_bytes=64)
         picked = {}
-        update_one = [keep.tile([P, BLOCKS, CHUNK], F32, name=f"update{c}", align_bytes=64) for c in range(2)]
-        update_two = keep.tile([P, BLOCKS, 2 * CHUNK], F32, name="update2", align_bytes=64)
-        update = [update_one[0][:], update_one[1][:], update_two[:, :, 0:CHUNK], update_two[:, :, CHUNK:]]
+        update = keep.tile([P, BLOCKS, S], F32, name="update", align_bytes=64)
 
         def deal_w1(g):
             source = w1raw[g][:].rearrange("p j (m t) -> p m j t", t=PACK)
@@ -119,8 +115,7 @@ def tile_picked_modres_mlpgelu_p_kernel(tc, x_words, x_scales, gate, res, w1, w2
 
         gate_ps = psum.tile([P, P], F32, name="gate_ps", tag="turn1")
         nc.tensor.transpose(gate_ps[:], gate_rows[:], ident[:])
-        nc.scalar.copy(gate_first[:], gate_ps[:, 0:1])
-        nc.scalar.copy(gate_rest[:], gate_ps[:, 1:CHUNKS])
+        nc.scalar.copy(gate_cols[:], gate_ps[:, 0:CHUNKS])
 
         xg.append(keep.tile([P, S], U32, name="xg1", align_bytes=64))
 
@@ -164,12 +159,12 @@ def tile_picked_modres_mlpgelu_p_kernel(tc, x_words, x_scales, gate, res, w1, w2
             nc.tensor.matmul_mx(
                 out=y[:], lhsT=hc[c][:].bitcast(FP8X4), lhsT_scale=hs[c][:], rhs=w2c[:].bitcast(FP8X4), rhs_scale=w2s[:], start=True, stop=True
             )
-            gated[c] = keep.tile([P, N], F32, name=f"gated{c}", tag=f"gated{c % 2}", align_bytes=64)
-            nc.scalar.activation(gated[c][:], y[:], ACT.Copy, scale=gate_cols[c])
+            gated[c] = keep.tile([P, N], F32, name=f"gated{c}", align_bytes=64)
+            nc.scalar.activation(gated[c][:], y[:], ACT.Copy, scale=gate_cols[:, c : c + 1])
             turned = psum.tile([P, BLOCKS, CHUNK], F32, name=f"turn{c}", tag=f"turn{c % 2}")
             for b in range(BLOCKS):
                 nc.tensor.transpose(turned[:, b, :], gated[c][:, b * P : (b + 1) * P], ident[:])
-            nc.scalar.copy(update[c], turned[:])
+            nc.scalar.copy(update[:, :, c * CHUNK : (c + 1) * CHUNK], turned[:])
 
         def look_up(b, tag):
             picked[b] = keep.tile([P, S], F32, name=f"picked{b}", tag=tag, align_bytes=64)
@@ -178,7 +173,7 @@ def tile_picked_modres_mlpgelu_p_kernel(tc, x_words, x_scales, gate, res, w1, w2
         def put(b, c0, c1):
             ent = slice(c0 * CHUNK, c1 * CHUNK)
             lists = offsets[:, c0 * CHUNK // LANES : c1 * CHUNK // LANES]
-            nc.vector.tensor_tensor(window[b][:].indirect(lists), (update_one[c0] if c1 - c0 == 1 else update_two)[:, b, :], picked[b][:, ent], ADD)
+            nc.vector.tensor_tensor(window[b][:].indirect(lists), update[:, b, ent], picked[b][:, ent], ADD)
 
         hidden(0)
         first_product(2, 0)
@@ -188,7 +183,7 @@ def tile_picked_modres_mlpgelu_p_kernel(tc, x_words, x_scales, gate, res, w1, w2
         w2c = keep.tile([P, N], U32, name="w2c", align_bytes=64)
         nc.vector.quantize_mx(out=w2c[:].bitcast(FP8X4), scales=w2s[:], in_=w2g[:].rearrange("p n j -> p (n j)"))
         second(0)
-        look_up(0, "hidden0")
+        look_up(0, "picked0")
         hidden(2)
         quantise_hidden(1)
         second(1)
@@ -201,8 +196,7 @@ def tile_picked_modres_mlpgelu_p_kernel(tc, x_words, x_scales, gate, res, w1, w2
         put(0, 0, 1)
         put(1, 0, 1)
         put(0, 1, 2)
-        put(1, 1, 2)
+        put(1, 1, 4)
+        nc.sync.dma_start(out=out[P : 2 * P, :], in_=window[1][:])
         put(0, 2, 4)
         nc.sync.dma_start(out=out[0:P, :], in_=window[0][:])
-        put(1, 2, 4)
-        nc.sync.dma_start(out=out[P : 2 * P, :], in_=window[1][:])

@@ -1,7 +1,6 @@
 from contextlib import ExitStack
 
 import concourse.mybir as mybir
-from concourse.masks import make_identity
 
 K, T, S, H, N = 1024, 1024, 512, 512, 256
 FLOPS = 2 * S * (K * H + H * N)
@@ -15,6 +14,7 @@ U8 = mybir.dt.uint8
 FP8X4 = mybir.dt.float8_e4m3fn_x4
 ACT = mybir.ActivationFunctionType
 ADD = mybir.AluOpType.add
+MULT = mybir.AluOpType.mult
 
 P = 128
 PACK = 4
@@ -40,13 +40,11 @@ def tile_picked_modres_mlpgelu_p_kernel(tc, x_words, x_scales, gate, res, w1, w2
         w1raw = [keep.tile([P, PACK, PACK * (m1 - m0)], F32, name=f"w1raw{i}", align_bytes=64) for i, (g, m0, m1) in enumerate(pieces)]
         w2raw = keep.tile([P, PACK, N], F32, name="w2raw", align_bytes=64)
         window = [keep.tile([P, T], F32, name=f"window{b}", align_bytes=64) for b in range(BLOCKS)]
-        gate_rows = keep.tile([P, CHUNK], F32, name="gate_rows", align_bytes=64)
-        ident = keep.tile([P, P], F32, name="ident", align_bytes=64)
+        gate_all = keep.tile([P, S], F32, name="gate_all", align_bytes=64)
         warm_in = keep.tile([P, 8], F32, name="warm_in", align_bytes=64)
         warm_out = keep.tile([P, 8], F32, name="warm_out", align_bytes=64)
 
         nc.gpsimd.memset(xs[:].bitcast(I32), 0)
-        nc.gpsimd.memset(gate_rows[:], 0.0)
         nc.vector.memset(warm_in[:], 0.0)
 
         def words(g):
@@ -62,16 +60,15 @@ def tile_picked_modres_mlpgelu_p_kernel(tc, x_words, x_scales, gate, res, w1, w2
                 out=xs[32 * q : 32 * q + 4 * PASSES, :].bitcast(I32),
                 in_=x_scales[:, 4 * q : 4 * q + 4, :].bitcast(I32),
             )
-        nc.sync.dma_start(out=gate_rows[0:CHUNKS, :], in_=gate[0].rearrange("(c n) -> c n", n=CHUNK))
         for i, (g, m0, m1) in enumerate(pieces):
             nc.sync.dma_start(out=w1raw[i][:], in_=rows(w1, g)[:, :, PACK * m0 : PACK * m1])
         nc.sync.dma_start(out=xw[1][:], in_=words(1))
         nc.sync.dma_start(out=w2raw[:], in_=rows(w2, 0))
-        for b in range(BLOCKS):
-            nc.sync.dma_start(out=window[b][:], in_=res[b * P : (b + 1) * P, :])
+        nc.sync.dma_start(out=window[1][:], in_=res[P : 2 * P, :])
+        nc.sync.dma_start(out=gate_all[:], in_=gate)
+        nc.sync.dma_start(out=window[0][:], in_=res[0:P, :])
 
         nc.scalar.activation(warm_out[:], warm_in[:], ACT.Gelu_apprx_tanh)
-        make_identity(nc, ident[:])
 
         xg = [keep.tile([P, S], U32, name="xg0", align_bytes=64)]
         xsg = keep.tile([P, S], U8, name="xsg", align_bytes=64)
@@ -79,9 +76,8 @@ def tile_picked_modres_mlpgelu_p_kernel(tc, x_words, x_scales, gate, res, w1, w2
         w1c = [keep.tile([P, H], U32, name=f"w1c{g}", align_bytes=64) for g in range(PASSES)]
         w1s = [keep.tile([P, H], U8, name=f"w1s{g}", align_bytes=64) for g in range(PASSES)]
         w2s = keep.tile([P, N], U8, name="w2s", align_bytes=64)
-        gate_cols = keep.tile([P, CHUNKS], F32, name="gate_cols", align_bytes=64)
-        picked = {}
-        update = keep.tile([P, BLOCKS, S], F32, name="update", align_bytes=64)
+        picked = [keep.tile([P, S], F32, name=f"picked{b}", align_bytes=64) for b in range(BLOCKS)]
+        total = keep.tile([P, S], F32, name="total", align_bytes=64)
 
         def deal_w1(g):
             source = w1raw[g][:].rearrange("p j (m t) -> p m j t", t=PACK)
@@ -113,10 +109,6 @@ def tile_picked_modres_mlpgelu_p_kernel(tc, x_words, x_scales, gate, res, w1, w2
         nc.vector.tensor_copy(xg[0][:], xw[0][:].bitcast(U32).indirect(offsets[:]))
         nc.vector.tensor_copy(xsg[:], xs[:].indirect(offsets[:]))
 
-        gate_ps = psum.tile([P, P], F32, name="gate_ps", tag="turn1")
-        nc.tensor.transpose(gate_ps[:], gate_rows[:], ident[:])
-        nc.scalar.copy(gate_cols[:], gate_ps[:, 0:CHUNKS])
-
         xg.append(keep.tile([P, S], U32, name="xg1", align_bytes=64))
 
         def gather_second_pass(c0, c1):
@@ -135,68 +127,88 @@ def tile_picked_modres_mlpgelu_p_kernel(tc, x_words, x_scales, gate, res, w1, w2
         gather_second_pass(1, 2)
         gather_second_pass(2, 4)
 
-        w2g = keep.tile([P, N, PACK], BF16, name="w2g", align_bytes=64)
+        def lists(c0, c1):
+            return offsets[:, c0 * CHUNK // LANES : c1 * CHUNK // LANES]
+
+        def span(c0, c1):
+            return slice(c0 * CHUNK, c1 * CHUNK)
+
+        def look_up(b, c0, c1):
+            nc.scalar.activation(picked[b][:, span(c0, c1)], window[b][:].indirect(lists(c0, c1)), ACT.Copy)
+
+        w2g = keep.tile([P, N, PACK], BF16, name="w2g", tag="w2g", align_bytes=64)
         nc.vector.tensor_copy(
             w2g[:].rearrange("p (c i) j -> p c j i", i=4),
             w2raw[:].rearrange("p j (c i) -> p c j i", i=4),
         )
 
         hg = {}
-        hc = [keep.tile([P, CHUNK], U32, name=f"hc{c}", align_bytes=64) for c in range(CHUNKS)]
-        hs = [keep.tile([P, CHUNK], U8, name=f"hs{c}", align_bytes=64) for c in range(CHUNKS)]
-        gated = {}
+        hc = keep.tile([P, S], U32, name="hc", align_bytes=64)
+        hs = keep.tile([P, S], U8, name="hs", align_bytes=64)
+        w2c = keep.tile([P, N], U32, name="w2c", align_bytes=64)
 
-        def hidden(c):
+        def hidden(c, tag):
             first_product(c, 1)
-            hg[c] = keep.tile([P, CHUNK, PACK], BF16, name=f"hg{c}", tag=f"hidden{c}", align_bytes=64)
+            hg[c] = keep.tile([P, CHUNK, PACK], BF16, name=f"hg{c}", tag=tag, align_bytes=64)
             nc.scalar.activation(hg[c][:], acc[c][:].rearrange("p t n -> p n t"), ACT.Gelu_apprx_tanh)
 
         def quantise_hidden(c):
-            nc.vector.quantize_mx(out=hc[c][:].bitcast(FP8X4), scales=hs[c][:], in_=hg[c][:].rearrange("p n t -> p (n t)"))
+            nc.vector.quantize_mx(out=hc[:, span(c, c + 1)].bitcast(FP8X4), scales=hs[:, span(c, c + 1)], in_=hg[c][:].rearrange("p n t -> p (n t)"))
 
-        def second(c):
-            y = psum.tile([P, N], F32, name=f"y{c}", tag=f"y{c % 2}")
+        def second(y, b, c0, c1):
+            cols = slice(b * P, (b + 1) * P)
             nc.tensor.matmul_mx(
-                out=y[:], lhsT=hc[c][:].bitcast(FP8X4), lhsT_scale=hs[c][:], rhs=w2c[:].bitcast(FP8X4), rhs_scale=w2s[:], start=True, stop=True
+                out=y,
+                lhsT=w2c[:, cols].bitcast(FP8X4),
+                lhsT_scale=w2s[:, cols],
+                rhs=hc[:, span(c0, c1)].bitcast(FP8X4),
+                rhs_scale=hs[:, span(c0, c1)],
+                start=True,
+                stop=True,
             )
-            gated[c] = keep.tile([P, N], F32, name=f"gated{c}", align_bytes=64)
-            nc.scalar.activation(gated[c][:], y[:], ACT.Copy, scale=gate_cols[:, c : c + 1])
-            turned = psum.tile([P, BLOCKS, CHUNK], F32, name=f"turn{c}", tag=f"turn{c % 2}")
-            for b in range(BLOCKS):
-                nc.tensor.transpose(turned[:, b, :], gated[c][:, b * P : (b + 1) * P], ident[:])
-            nc.scalar.copy(update[:, :, c * CHUNK : (c + 1) * CHUNK], turned[:])
 
-        def look_up(b, tag):
-            picked[b] = keep.tile([P, S], F32, name=f"picked{b}", tag=tag, align_bytes=64)
-            nc.vector.tensor_copy(picked[b][:], window[b][:].indirect(offsets[:]))
+        def put_vector(values, c0, c1):
+            nc.vector.tensor_tensor(window[1][:].indirect(lists(c0, c1)), values, picked[1][:, span(c0, c1)], ADD)
 
-        def put(b, c0, c1):
-            ent = slice(c0 * CHUNK, c1 * CHUNK)
-            lists = offsets[:, c0 * CHUNK // LANES : c1 * CHUNK // LANES]
-            nc.vector.tensor_tensor(window[b][:].indirect(lists), update[:, b, ent], picked[b][:, ent], ADD)
+        def put_scalar(c0, c1):
+            nc.scalar.activation(window[0][:].indirect(lists(c0, c1)), total[:, span(c0, c1)], ACT.Copy)
 
-        hidden(0)
+        def gated(values, y, c0, c1):
+            nc.vector.tensor_tensor(values, y, gate_all[:, span(c0, c1)], MULT)
+
+        def add(values, c0, c1):
+            nc.vector.tensor_tensor(total[:, span(c0, c1)], values, picked[0][:, span(c0, c1)], ADD)
+
+        y_a = [psum.tile([P, 2 * CHUNK], F32, name=f"y_a{h}", tag=f"y{h}") for h in range(2)]
+        y_b = psum.tile([P, S], F32, name="y_b", tag="y2")
+        update_a = [keep.tile([P, 2 * CHUNK], F32, name=f"update_a{h}", tag=f"gated{h}", align_bytes=64) for h in range(2)]
+
+        hidden(0, "hidden0")
         first_product(2, 0)
-        hidden(1)
+        hidden(1, "hidden1")
         first_product(3, 0)
         quantise_hidden(0)
-        w2c = keep.tile([P, N], U32, name="w2c", align_bytes=64)
         nc.vector.quantize_mx(out=w2c[:].bitcast(FP8X4), scales=w2s[:], in_=w2g[:].rearrange("p n j -> p (n j)"))
-        second(0)
-        look_up(0, "picked0")
-        hidden(2)
+        hidden(2, "hidden2")
+        nc.vector.tensor_copy(picked[1][:], window[1][:].indirect(offsets[:]))
         quantise_hidden(1)
-        second(1)
-        look_up(1, "picked1")
-        hidden(3)
+        second(y_a[0][:], 0, 0, 2)
+        hidden(3, "hidden3")
         quantise_hidden(2)
-        second(2)
         quantise_hidden(3)
-        second(3)
-        put(0, 0, 1)
-        put(1, 0, 1)
-        put(0, 1, 2)
-        put(1, 1, 4)
-        nc.sync.dma_start(out=out[P : 2 * P, :], in_=window[1][:])
-        put(0, 2, 4)
+        gated(update_a[0][:], y_a[0][:], 0, 2)
+        second(y_a[1][:], 0, 2, 4)
+        second(y_b[:], 1, 0, 4)
+        look_up(0, 0, 2)
+        look_up(0, 2, 4)
+        add(update_a[0][:], 0, 2)
+        gated(update_a[1][:], y_a[1][:], 2, 4)
+        add(update_a[1][:], 2, 4)
+        put_scalar(0, 2)
+        put_scalar(2, 4)
+        update_b = keep.tile([P, S], F32, name="update_b", tag="gated0", align_bytes=64)
+        gated(update_b[:], y_b[:], 0, 4)
+        put_vector(update_b[:, span(0, 2)], 0, 2)
+        put_vector(update_b[:, span(2, 4)], 2, 4)
         nc.sync.dma_start(out=out[0:P, :], in_=window[0][:])
+        nc.sync.dma_start(out=out[P : 2 * P, :], in_=window[1][:])

@@ -73,10 +73,10 @@ def tile_picked_modres_mlpgelu_p_kernel(tc, x_words, x_scales, gate, res, w1, w2
         xg = [keep.tile([P, S], U32, name="xg0", align_bytes=64)]
         xsg = keep.tile([P, S], U8, name="xsg", align_bytes=64)
         w1g = [keep.tile([P, PACK, P, PACK], BF16, name=f"w1g{g}", align_bytes=64) for g in range(PASSES)]
-        w1c = [keep.tile([P, H], U32, name=f"w1c{g}", align_bytes=64) for g in range(PASSES)]
+        w1c = [keep.tile([P, H], U32, name=f"w1c{g}", tag=f"w1c{g}", align_bytes=64) for g in range(PASSES)]
         w1s = [keep.tile([P, H], U8, name=f"w1s{g}", align_bytes=64) for g in range(PASSES)]
         w2s = keep.tile([P, N], U8, name="w2s", align_bytes=64)
-        picked = [keep.tile([P, S], F32, name=f"picked{b}", align_bytes=64) for b in range(BLOCKS)]
+        picked_a = [keep.tile([P, 2 * CHUNK], F32, name=f"picked_a{h}", tag=f"picked_a{h}", align_bytes=64) for h in range(2)]
         total = keep.tile([P, S], F32, name="total", align_bytes=64)
 
         def deal_w1(g):
@@ -133,8 +133,8 @@ def tile_picked_modres_mlpgelu_p_kernel(tc, x_words, x_scales, gate, res, w1, w2
         def span(c0, c1):
             return slice(c0 * CHUNK, c1 * CHUNK)
 
-        def look_up(b, c0, c1):
-            nc.scalar.activation(picked[b][:, span(c0, c1)], window[b][:].indirect(lists(c0, c1)), ACT.Copy)
+        def look_up(h):
+            nc.scalar.activation(picked_a[h][:], window[0][:].indirect(lists(2 * h, 2 * h + 2)), ACT.Copy)
 
         w2g = keep.tile([P, N, PACK], BF16, name="w2g", tag="w2g", align_bytes=64)
         nc.vector.tensor_copy(
@@ -142,18 +142,19 @@ def tile_picked_modres_mlpgelu_p_kernel(tc, x_words, x_scales, gate, res, w1, w2
             w2raw[:].rearrange("p j (c i) -> p c j i", i=4),
         )
 
-        hg = {}
+        hg = keep.tile([P, CHUNKS, CHUNK, PACK], BF16, name="hg", align_bytes=64)
         hc = keep.tile([P, S], U32, name="hc", align_bytes=64)
         hs = keep.tile([P, S], U8, name="hs", align_bytes=64)
         w2c = keep.tile([P, N], U32, name="w2c", align_bytes=64)
 
-        def hidden(c, tag):
+        def hidden(c):
             first_product(c, 1)
-            hg[c] = keep.tile([P, CHUNK, PACK], BF16, name=f"hg{c}", tag=tag, align_bytes=64)
-            nc.scalar.activation(hg[c][:], acc[c][:].rearrange("p t n -> p n t"), ACT.Gelu_apprx_tanh)
+            nc.scalar.activation(hg[:, c], acc[c][:].rearrange("p t n -> p n t"), ACT.Gelu_apprx_tanh)
 
-        def quantise_hidden(c):
-            nc.vector.quantize_mx(out=hc[:, span(c, c + 1)].bitcast(FP8X4), scales=hs[:, span(c, c + 1)], in_=hg[c][:].rearrange("p n t -> p (n t)"))
+        def quantise_hidden(c0, c1):
+            nc.vector.quantize_mx(
+                out=hc[:, span(c0, c1)].bitcast(FP8X4), scales=hs[:, span(c0, c1)], in_=hg[:, c0:c1].rearrange("p c n t -> p (c n t)")
+            )
 
         def second(y, b, c0, c1):
             cols = slice(b * P, (b + 1) * P)
@@ -168,7 +169,7 @@ def tile_picked_modres_mlpgelu_p_kernel(tc, x_words, x_scales, gate, res, w1, w2
             )
 
         def put_vector(values, c0, c1):
-            nc.vector.tensor_tensor(window[1][:].indirect(lists(c0, c1)), values, picked[1][:, span(c0, c1)], ADD)
+            nc.vector.tensor_tensor(window[1][:].indirect(lists(c0, c1)), values, picked_b[:, span(c0, c1)], ADD)
 
         def put_scalar(c0, c1):
             nc.scalar.activation(window[0][:].indirect(lists(c0, c1)), total[:, span(c0, c1)], ACT.Copy)
@@ -176,39 +177,41 @@ def tile_picked_modres_mlpgelu_p_kernel(tc, x_words, x_scales, gate, res, w1, w2
         def gated(values, y, c0, c1):
             nc.vector.tensor_tensor(values, y, gate_all[:, span(c0, c1)], MULT)
 
-        def add(values, c0, c1):
-            nc.vector.tensor_tensor(total[:, span(c0, c1)], values, picked[0][:, span(c0, c1)], ADD)
+        def add(values, h):
+            nc.vector.tensor_tensor(total[:, span(2 * h, 2 * h + 2)], values, picked_a[h][:], ADD)
 
         y_a = [psum.tile([P, 2 * CHUNK], F32, name=f"y_a{h}", tag=f"y{h}") for h in range(2)]
         y_b = psum.tile([P, S], F32, name="y_b", tag="y2")
-        update_a = [keep.tile([P, 2 * CHUNK], F32, name=f"update_a{h}", tag=f"gated{h}", align_bytes=64) for h in range(2)]
+        update_a = [keep.tile([P, 2 * CHUNK], F32, name="update_a0", tag="gated", align_bytes=64)]
 
-        hidden(0, "hidden0")
+        hidden(0)
         first_product(2, 0)
-        hidden(1, "hidden1")
+        hidden(1)
         first_product(3, 0)
-        quantise_hidden(0)
+        quantise_hidden(0, 1)
         nc.vector.quantize_mx(out=w2c[:].bitcast(FP8X4), scales=w2s[:], in_=w2g[:].rearrange("p n j -> p (n j)"))
-        hidden(2, "hidden2")
-        nc.vector.tensor_copy(picked[1][:], window[1][:].indirect(offsets[:]))
-        quantise_hidden(1)
+        hidden(2)
+        quantise_hidden(1, 2)
         second(y_a[0][:], 0, 0, 2)
-        hidden(3, "hidden3")
-        quantise_hidden(2)
-        quantise_hidden(3)
+        second(y_b[:, span(0, 2)], 1, 0, 2)
+        hidden(3)
+        picked_b = keep.tile([P, S], F32, name="picked_b", tag="w1c1", align_bytes=64)
+        nc.vector.tensor_copy(picked_b[:, span(1, 4)], window[1][:].indirect(lists(1, 4)))
+        nc.scalar.activation(picked_b[:, span(0, 1)], window[1][:].indirect(lists(0, 1)), ACT.Copy)
+        quantise_hidden(2, 4)
         gated(update_a[0][:], y_a[0][:], 0, 2)
         second(y_a[1][:], 0, 2, 4)
-        second(y_b[:], 1, 0, 4)
-        look_up(0, 0, 2)
-        look_up(0, 2, 4)
-        add(update_a[0][:], 0, 2)
+        second(y_b[:, span(2, 4)], 1, 2, 4)
+        look_up(0)
+        look_up(1)
+        add(update_a[0][:], 0)
+        update_a.append(keep.tile([P, 2 * CHUNK], F32, name="update_a1", tag="gated", align_bytes=64))
         gated(update_a[1][:], y_a[1][:], 2, 4)
-        add(update_a[1][:], 2, 4)
+        add(update_a[1][:], 1)
         put_scalar(0, 2)
         put_scalar(2, 4)
-        update_b = keep.tile([P, S], F32, name="update_b", tag="gated0", align_bytes=64)
+        update_b = keep.tile([P, S], F32, name="update_b", tag="picked_a0", align_bytes=64)
         gated(update_b[:], y_b[:], 0, 4)
-        put_vector(update_b[:, span(0, 2)], 0, 2)
-        put_vector(update_b[:, span(2, 4)], 2, 4)
+        put_vector(update_b[:], 0, 4)
         nc.sync.dma_start(out=out[0:P, :], in_=window[0][:])
         nc.sync.dma_start(out=out[P : 2 * P, :], in_=window[1][:])

@@ -64,9 +64,9 @@ def tile_picked_modres_mlpgelu_p_kernel(tc, x_words, x_scales, gate, res, w1, w2
             nc.sync.dma_start(out=w1raw[i][:], in_=rows(w1, g)[:, :, PACK * m0 : PACK * m1])
         nc.sync.dma_start(out=xw[1][:], in_=words(1))
         nc.sync.dma_start(out=w2raw[:], in_=rows(w2, 0))
-        nc.sync.dma_start(out=window[1][:], in_=res[P : 2 * P, :])
+        for b in range(BLOCKS):
+            nc.sync.dma_start(out=window[b][:], in_=res[b * P : (b + 1) * P, :])
         nc.sync.dma_start(out=gate_all[:], in_=gate)
-        nc.sync.dma_start(out=window[0][:], in_=res[0:P, :])
 
         nc.scalar.activation(warm_out[:], warm_in[:], ACT.Gelu_apprx_tanh)
 
@@ -76,7 +76,7 @@ def tile_picked_modres_mlpgelu_p_kernel(tc, x_words, x_scales, gate, res, w1, w2
         w1c = [keep.tile([P, H], U32, name=f"w1c{g}", tag=f"w1c{g}", align_bytes=64) for g in range(PASSES)]
         w1s = [keep.tile([P, H], U8, name=f"w1s{g}", align_bytes=64) for g in range(PASSES)]
         w2s = keep.tile([P, N], U8, name="w2s", align_bytes=64)
-        picked_a = [keep.tile([P, 2 * CHUNK], F32, name=f"picked_a{h}", tag=f"picked_a{h}", align_bytes=64) for h in range(2)]
+        picked_b = keep.tile([P, S], F32, name="picked_b", align_bytes=64)
         total = keep.tile([P, S], F32, name="total", align_bytes=64)
 
         def deal_w1(g):
@@ -133,9 +133,6 @@ def tile_picked_modres_mlpgelu_p_kernel(tc, x_words, x_scales, gate, res, w1, w2
         def span(c0, c1):
             return slice(c0 * CHUNK, c1 * CHUNK)
 
-        def look_up(h):
-            nc.scalar.activation(picked_a[h][:], window[0][:].indirect(lists(2 * h, 2 * h + 2)), ACT.Copy)
-
         w2g = keep.tile([P, N, PACK], BF16, name="w2g", tag="w2g", align_bytes=64)
         nc.vector.tensor_copy(
             w2g[:].rearrange("p (c i) j -> p c j i", i=4),
@@ -178,11 +175,12 @@ def tile_picked_modres_mlpgelu_p_kernel(tc, x_words, x_scales, gate, res, w1, w2
             nc.vector.tensor_tensor(values, y, gate_all[:, span(c0, c1)], MULT)
 
         def add(values, h):
-            nc.vector.tensor_tensor(total[:, span(2 * h, 2 * h + 2)], values, picked_a[h][:], ADD)
+            nc.vector.tensor_tensor(total[:, span(2 * h, 2 * h + 2)], values, picked_a[:, span(2 * h, 2 * h + 2)], ADD)
 
         y_a = [psum.tile([P, 2 * CHUNK], F32, name=f"y_a{h}", tag=f"y{h}") for h in range(2)]
         y_b = psum.tile([P, S], F32, name="y_b", tag="y2")
-        update_a = [keep.tile([P, 2 * CHUNK], F32, name="update_a0", tag="gated", align_bytes=64)]
+        update_a = [keep.tile([P, 2 * CHUNK], F32, name=f"update_a{h}", align_bytes=64) for h in range(2)]
+        update_b = keep.tile([P, S], F32, name="update_b", align_bytes=64)
 
         hidden(0)
         first_product(2, 0)
@@ -195,23 +193,20 @@ def tile_picked_modres_mlpgelu_p_kernel(tc, x_words, x_scales, gate, res, w1, w2
         second(y_a[0][:], 0, 0, 2)
         second(y_b[:, span(0, 2)], 1, 0, 2)
         hidden(3)
-        picked_b = keep.tile([P, S], F32, name="picked_b", tag="w1c1", align_bytes=64)
-        nc.vector.tensor_copy(picked_b[:, span(1, 4)], window[1][:].indirect(lists(1, 4)))
-        nc.scalar.activation(picked_b[:, span(0, 1)], window[1][:].indirect(lists(0, 1)), ACT.Copy)
+        picked_a = keep.tile([P, S], F32, name="picked_a", tag="w1c1", align_bytes=64)
+        nc.vector.tensor_copy(picked_a[:, span(0, 3)], window[0][:].indirect(lists(0, 3)))
+        nc.scalar.activation(picked_a[:, span(3, 4)], window[0][:].indirect(lists(3, 4)), ACT.Copy)
+        nc.scalar.activation(picked_b[:], window[1][:].indirect(offsets[:]), ACT.Copy)
         quantise_hidden(2, 4)
         gated(update_a[0][:], y_a[0][:], 0, 2)
         second(y_a[1][:], 0, 2, 4)
         second(y_b[:, span(2, 4)], 1, 2, 4)
-        look_up(0)
-        look_up(1)
         add(update_a[0][:], 0)
-        update_a.append(keep.tile([P, 2 * CHUNK], F32, name="update_a1", tag="gated", align_bytes=64))
         gated(update_a[1][:], y_a[1][:], 2, 4)
         add(update_a[1][:], 1)
+        gated(update_b[:], y_b[:], 0, 4)
         put_scalar(0, 2)
         put_scalar(2, 4)
-        update_b = keep.tile([P, S], F32, name="update_b", tag="picked_a0", align_bytes=64)
-        gated(update_b[:], y_b[:], 0, 4)
         put_vector(update_b[:], 0, 4)
         nc.sync.dma_start(out=out[0:P, :], in_=window[0][:])
         nc.sync.dma_start(out=out[P : 2 * P, :], in_=window[1][:])

@@ -179,8 +179,7 @@ def tile_picked_modres_mlpgelu_p_kernel(tc, x_words, x_scales, gate, res, w1, w2
 
         y_a = [psum.tile([P, 2 * CHUNK], F32, name=f"y_a{h}", tag=f"y{h}") for h in range(2)]
         y_b = psum.tile([P, S], F32, name="y_b", tag="y2")
-        update_a = [keep.tile([P, 2 * CHUNK], F32, name=f"update_a{h}", align_bytes=64) for h in range(2)]
-        update_b = keep.tile([P, S], F32, name="update_b", align_bytes=64)
+        early = keep.tile([P, 2 * CHUNK], F32, name="early", tag="gated", align_bytes=64)
 
         hidden(0)
         first_product(2, 0)
@@ -198,15 +197,16 @@ def tile_picked_modres_mlpgelu_p_kernel(tc, x_words, x_scales, gate, res, w1, w2
         nc.scalar.activation(picked_a[:, span(3, 4)], window[0][:].indirect(lists(3, 4)), ACT.Copy)
         nc.scalar.activation(picked_b[:], window[1][:].indirect(offsets[:]), ACT.Copy)
         quantise_hidden(2, 4)
-        gated(update_a[0][:], y_a[0][:], 0, 2)
+        gated(early[:], y_a[0][:], 0, 2)
         second(y_a[1][:], 0, 2, 4)
         second(y_b[:, span(2, 4)], 1, 2, 4)
-        add(update_a[0][:], 0)
-        gated(update_a[1][:], y_a[1][:], 2, 4)
-        add(update_a[1][:], 1)
-        gated(update_b[:], y_b[:], 0, 4)
+        add(early[:], 0)
+        late = keep.tile([P, 6 * CHUNK], F32, name="late", tag="gated", align_bytes=64)
+        gated(late[:, span(4, 6)], y_a[1][:], 2, 4)
+        gated(late[:, span(0, 4)], y_b[:], 0, 4)
+        add(late[:, span(4, 6)], 1)
         put_scalar(0, 2)
         put_scalar(2, 4)
-        put_vector(update_b[:], 0, 4)
+        put_vector(late[:, span(0, 4)], 0, 4)
         nc.sync.dma_start(out=out[0:P, :], in_=window[0][:])
         nc.sync.dma_start(out=out[P : 2 * P, :], in_=window[1][:])

@@ -177,9 +177,10 @@ def tile_picked_modres_mlpgelu_p_kernel(tc, x_words, x_scales, gate, res, w1, w2
         def add(values, h):
             nc.vector.tensor_tensor(total[:, span(2 * h, 2 * h + 2)], values, picked_a[:, span(2 * h, 2 * h + 2)], ADD)
 
-        y_a = [psum.tile([P, 2 * CHUNK], F32, name=f"y_a{h}", tag=f"y{h}") for h in range(2)]
-        y_b = psum.tile([P, S], F32, name="y_b", tag="y2")
-        early = keep.tile([P, 2 * CHUNK], F32, name="early", tag="gated", align_bytes=64)
+        y_a = [psum.tile([P, 2 * CHUNK], F32, name="y_a0", tag="y_a")]
+        y_b = [psum.tile([P, 2 * CHUNK], F32, name=f"y_b{h}", tag=f"y_b{h}") for h in range(2)]
+        gated_a = keep.tile([P, S], F32, name="gated_a", align_bytes=64)
+        gated_b = keep.tile([P, S], F32, name="gated_b", align_bytes=64)
 
         hidden(0)
         first_product(2, 0)
@@ -190,23 +191,24 @@ def tile_picked_modres_mlpgelu_p_kernel(tc, x_words, x_scales, gate, res, w1, w2
         hidden(2)
         quantise_hidden(1, 2)
         second(y_a[0][:], 0, 0, 2)
-        second(y_b[:, span(0, 2)], 1, 0, 2)
+        second(y_b[0][:], 1, 0, 2)
         hidden(3)
         picked_a = keep.tile([P, S], F32, name="picked_a", tag="w1c1", align_bytes=64)
         nc.vector.tensor_copy(picked_a[:, span(0, 3)], window[0][:].indirect(lists(0, 3)))
         nc.scalar.activation(picked_a[:, span(3, 4)], window[0][:].indirect(lists(3, 4)), ACT.Copy)
         nc.scalar.activation(picked_b[:], window[1][:].indirect(offsets[:]), ACT.Copy)
         quantise_hidden(2, 4)
-        gated(early[:], y_a[0][:], 0, 2)
+        gated(gated_a[:, span(0, 2)], y_a[0][:], 0, 2)
+        gated(gated_b[:, span(0, 2)], y_b[0][:], 0, 2)
+        add(gated_a[:, span(0, 2)], 0)
+        y_a.append(psum.tile([P, 2 * CHUNK], F32, name="y_a1", tag="y_a"))
         second(y_a[1][:], 0, 2, 4)
-        second(y_b[:, span(2, 4)], 1, 2, 4)
-        add(early[:], 0)
-        late = keep.tile([P, 6 * CHUNK], F32, name="late", tag="gated", align_bytes=64)
-        gated(late[:, span(4, 6)], y_a[1][:], 2, 4)
-        gated(late[:, span(0, 4)], y_b[:], 0, 4)
-        add(late[:, span(4, 6)], 1)
+        second(y_b[1][:], 1, 2, 4)
+        gated(gated_a[:, span(2, 4)], y_a[1][:], 2, 4)
+        gated(gated_b[:, span(2, 4)], y_b[1][:], 2, 4)
+        add(gated_a[:, span(2, 4)], 1)
         put_scalar(0, 2)
         put_scalar(2, 4)
-        put_vector(late[:, span(0, 4)], 0, 4)
+        put_vector(gated_b[:], 0, 4)
         nc.sync.dma_start(out=out[0:P, :], in_=window[0][:])
         nc.sync.dma_start(out=out[P : 2 * P, :], in_=window[1][:])

@@ -24,7 +24,6 @@ CHUNK = 128
 CHUNKS = S // CHUNK
 BLOCKS = N // P
 LANES = 16
-HALF = P // 2
 
 
 def tile_picked_modres_mlpgelu_p_kernel(tc, x_words, x_scales, gate, res, w1, w2, offs, out):
@@ -40,7 +39,7 @@ def tile_picked_modres_mlpgelu_p_kernel(tc, x_words, x_scales, gate, res, w1, w2
         w1raw = [keep.tile([P, PACK, PACK * (m1 - m0)], F32, name=f"w1raw{i}", align_bytes=64) for i, (g, m0, m1) in enumerate(pieces)]
         w2raw = keep.tile([P, PACK, N], F32, name="w2raw", align_bytes=64)
         window = [keep.tile([P, T], F32, name=f"window{b}", align_bytes=64) for b in range(BLOCKS)]
-        gate_all = keep.tile([P, S], F32, name="gate_all", align_bytes=64)
+        gate_half = [keep.tile([P, S // 2], F32, name=f"gate_half{h}", tag=f"gate_half{h}", align_bytes=64) for h in range(2)]
         warm_in = keep.tile([P, 8], F32, name="warm_in", align_bytes=64)
         warm_out = keep.tile([P, 8], F32, name="warm_out", align_bytes=64)
 
@@ -66,7 +65,8 @@ def tile_picked_modres_mlpgelu_p_kernel(tc, x_words, x_scales, gate, res, w1, w2
         nc.sync.dma_start(out=w2raw[:], in_=rows(w2, 0))
         for b in range(BLOCKS):
             nc.sync.dma_start(out=window[b][:], in_=res[b * P : (b + 1) * P, :])
-        nc.sync.dma_start(out=gate_all[:], in_=gate)
+        for h in range(2):
+            nc.sync.dma_start(out=gate_half[h][:], in_=gate[:, h * S // 2 : (h + 1) * S // 2])
 
         nc.scalar.activation(warm_out[:], warm_in[:], ACT.Gelu_apprx_tanh)
 
@@ -76,7 +76,11 @@ def tile_picked_modres_mlpgelu_p_kernel(tc, x_words, x_scales, gate, res, w1, w2
         w1c = [keep.tile([P, H], U32, name=f"w1c{g}", tag=f"w1c{g}", align_bytes=64) for g in range(PASSES)]
         w1s = [keep.tile([P, H], U8, name=f"w1s{g}", align_bytes=64) for g in range(PASSES)]
         w2s = keep.tile([P, N], U8, name="w2s", align_bytes=64)
-        picked_b = keep.tile([P, S], F32, name="picked_b", align_bytes=64)
+        terms = keep.tile([P, 11, CHUNK], F32, name="terms", align_bytes=64)
+
+        def slots(s0, s1):
+            return terms[:, s0:s1].rearrange("p s n -> p (s n)")
+
         total = keep.tile([P, S], F32, name="total", align_bytes=64)
 
         def deal_w1(g):
@@ -140,7 +144,7 @@ def tile_picked_modres_mlpgelu_p_kernel(tc, x_words, x_scales, gate, res, w1, w2
         )
 
         hg = keep.tile([P, CHUNKS, CHUNK, PACK], BF16, name="hg", align_bytes=64)
-        hc = keep.tile([P, S], U32, name="hc", align_bytes=64)
+        hc = [keep.tile([P, S // 2], U32, name="hc0", align_bytes=64)]
         hs = keep.tile([P, S], U8, name="hs", align_bytes=64)
         w2c = keep.tile([P, N], U32, name="w2c", align_bytes=64)
 
@@ -150,7 +154,7 @@ def tile_picked_modres_mlpgelu_p_kernel(tc, x_words, x_scales, gate, res, w1, w2
 
         def quantise_hidden(c0, c1):
             nc.vector.quantize_mx(
-                out=hc[:, span(c0, c1)].bitcast(FP8X4), scales=hs[:, span(c0, c1)], in_=hg[:, c0:c1].rearrange("p c n t -> p (c n t)")
+                out=hc[c0 // 2][:, span(c0 % 2, c0 % 2 + c1 - c0)].bitcast(FP8X4), scales=hs[:, span(c0, c1)], in_=hg[:, c0:c1].rearrange("p c n t -> p (c n t)")
             )
 
         def second(y, b, c0, c1):
@@ -159,28 +163,24 @@ def tile_picked_modres_mlpgelu_p_kernel(tc, x_words, x_scales, gate, res, w1, w2
                 out=y,
                 lhsT=w2c[:, cols].bitcast(FP8X4),
                 lhsT_scale=w2s[:, cols],
-                rhs=hc[:, span(c0, c1)].bitcast(FP8X4),
+                rhs=hc[c0 // 2][:].bitcast(FP8X4),
                 rhs_scale=hs[:, span(c0, c1)],
                 start=True,
                 stop=True,
             )
 
-        def put_vector(values, c0, c1):
-            nc.vector.tensor_tensor(window[1][:].indirect(lists(c0, c1)), values, picked_b[:, span(c0, c1)], ADD)
-
         def put_scalar(c0, c1):
             nc.scalar.activation(window[0][:].indirect(lists(c0, c1)), total[:, span(c0, c1)], ACT.Copy)
 
         def gated(values, y, c0, c1):
-            nc.vector.tensor_tensor(values, y, gate_all[:, span(c0, c1)], MULT)
+            nc.vector.tensor_tensor(values, y, gate_half[c0 // 2][:], MULT)
 
         def add(values, h):
-            nc.vector.tensor_tensor(total[:, span(2 * h, 2 * h + 2)], values, picked_a[:, span(2 * h, 2 * h + 2)], ADD)
+            nc.vector.tensor_tensor(total[:, span(2 * h, 2 * h + 2)], values, slots(3 + 2 * h, 5 + 2 * h), ADD)
 
-        y_a = [psum.tile([P, 2 * CHUNK], F32, name="y_a0", tag="y_a")]
+        y_a = [psum.tile([P, 2 * CHUNK], F32, name=f"y_a{h}", tag=f"y_a{h}") for h in range(2)]
         y_b = [psum.tile([P, 2 * CHUNK], F32, name=f"y_b{h}", tag=f"y_b{h}") for h in range(2)]
         gated_a = keep.tile([P, S], F32, name="gated_a", align_bytes=64)
-        gated_b = keep.tile([P, S], F32, name="gated_b", align_bytes=64)
 
         hidden(0)
         first_product(2, 0)
@@ -193,22 +193,24 @@ def tile_picked_modres_mlpgelu_p_kernel(tc, x_words, x_scales, gate, res, w1, w2
         second(y_a[0][:], 0, 0, 2)
         second(y_b[0][:], 1, 0, 2)
         hidden(3)
-        picked_a = keep.tile([P, S], F32, name="picked_a", tag="w1c1", align_bytes=64)
-        nc.vector.tensor_copy(picked_a[:, span(0, 3)], window[0][:].indirect(lists(0, 3)))
-        nc.scalar.activation(picked_a[:, span(3, 4)], window[0][:].indirect(lists(3, 4)), ACT.Copy)
-        nc.scalar.activation(picked_b[:], window[1][:].indirect(offsets[:]), ACT.Copy)
-        quantise_hidden(2, 4)
+        nc.vector.tensor_copy(slots(3, 6), window[0][:].indirect(lists(0, 3)))
+        nc.scalar.activation(slots(6, 7), window[0][:].indirect(lists(3, 4)), ACT.Copy)
+        nc.scalar.activation(slots(7, 10), window[1][:].indirect(lists(0, 3)), ACT.Copy)
         gated(gated_a[:, span(0, 2)], y_a[0][:], 0, 2)
-        gated(gated_b[:, span(0, 2)], y_b[0][:], 0, 2)
+        gated(slots(0, 2), y_b[0][:], 0, 2)
         add(gated_a[:, span(0, 2)], 0)
-        y_a.append(psum.tile([P, 2 * CHUNK], F32, name="y_a1", tag="y_a"))
+        hc.append(keep.tile([P, S // 2], U32, name="hc1", tag="gate_half0", align_bytes=64))
+        quantise_hidden(2, 4)
         second(y_a[1][:], 0, 2, 4)
         second(y_b[1][:], 1, 2, 4)
+        nc.vector.tensor_copy(slots(3, 4), window[1][:].indirect(lists(3, 4)))
         gated(gated_a[:, span(2, 4)], y_a[1][:], 2, 4)
-        gated(gated_b[:, span(2, 4)], y_b[1][:], 2, 4)
+        nc.vector.tensor_tensor(
+            terms[:, 2:11:8], y_b[1][:].rearrange("p (c n) -> p c n", c=2), gate_half[1][:].rearrange("p (c n) -> p c n", c=2), MULT
+        )
         add(gated_a[:, span(2, 4)], 1)
         put_scalar(0, 2)
         put_scalar(2, 4)
-        put_vector(gated_b[:], 0, 4)
+        nc.vector.tensor_tensor(window[1][:].indirect(offsets[:]), slots(0, 4), slots(7, 11), ADD)
         nc.sync.dma_start(out=out[0:P, :], in_=window[0][:])
         nc.sync.dma_start(out=out[P : 2 * P, :], in_=window[1][:])

@@ -193,8 +193,8 @@ def tile_picked_modres_mlpgelu_p_kernel(tc, x_words, x_scales, gate, res, w1, w2
         second(y_a[0][:], 0, 0, 2)
         second(y_b[0][:], 1, 0, 2)
         hidden(3)
-        nc.vector.tensor_copy(slots(3, 6), window[0][:].indirect(lists(0, 3)))
-        nc.scalar.activation(slots(6, 7), window[0][:].indirect(lists(3, 4)), ACT.Copy)
+        nc.vector.tensor_copy(slots(3, 5), window[0][:].indirect(lists(0, 2)))
+        nc.scalar.activation(slots(5, 7), window[0][:].indirect(lists(2, 4)), ACT.Copy)
         nc.scalar.activation(slots(7, 10), window[1][:].indirect(lists(0, 3)), ACT.Copy)
         gated(gated_a[:, span(0, 2)], y_a[0][:], 0, 2)
         gated(slots(0, 2), y_b[0][:], 0, 2)

from contextlib import ExitStack

import concourse.mybir as mybir

K, T, S, H, N = 1024, 1024, 512, 512, 256
FLOPS = 2 * S * (K * H + H * N)

F32 = mybir.dt.float32
BF16 = mybir.dt.bfloat16
I32 = mybir.dt.int32
U32 = mybir.dt.uint32
U16 = mybir.dt.uint16
U8 = mybir.dt.uint8
FP8X4 = mybir.dt.float8_e4m3fn_x4
ACT = mybir.ActivationFunctionType
ADD = mybir.AluOpType.add
MULT = mybir.AluOpType.mult

P = 128
PACK = 4
K_PASS = P * PACK
PASSES = K // K_PASS
CHUNK = 128
CHUNKS = S // CHUNK
BLOCKS = N // P
LANES = 16


def tile_picked_modres_mlpgelu_p_kernel(tc, x_words, x_scales, gate, res, w1, w2, offs, out):
    nc = tc.nc
    with ExitStack() as ctx:
        keep = ctx.enter_context(tc.tile_pool(name="keep", bufs=1))
        psum = ctx.enter_context(tc.psum_pool(name="psum", bufs=1))

        offsets = keep.tile([P, S // LANES], U16, name="offsets")
        xw = [keep.tile([P, T], I32, name=f"xw{g}", align_bytes=64) for g in range(PASSES)]
        xs = keep.tile([P, T], U8, name="xs", align_bytes=64)
        pieces = ((0, 0, P), (1, 0, P))
        w1raw = [keep.tile([P, PACK, PACK * (m1 - m0)], F32, name=f"w1raw{i}", align_bytes=64) for i, (g, m0, m1) in enumerate(pieces)]
        w2raw = keep.tile([P, PACK, N], F32, name="w2raw", align_bytes=64)
        window = [keep.tile([P, T], F32, name=f"window{b}", align_bytes=64) for b in range(BLOCKS)]
        gate_half = [keep.tile([P, S // 2], F32, name=f"gate_half{h}", tag=f"gate_half{h}", align_bytes=64) for h in range(2)]
        warm_in = keep.tile([P, 8], F32, name="warm_in", align_bytes=64)
        warm_out = keep.tile([P, 8], F32, name="warm_out", align_bytes=64)

        nc.gpsimd.memset(xs[:].bitcast(I32), 0)
        nc.vector.memset(warm_in[:], 0.0)

        def words(g):
            return x_words[g].rearrange("p c r -> p (c r)").bitcast(I32)

        def rows(w, g):
            return w[g * K_PASS : (g + 1) * K_PASS, :].rearrange("(p j) c -> p j c", j=PACK)

        nc.sync.dma_start(out=xw[0][:], in_=words(0))
        nc.sync.dma_start(offsets[:], offs)
        for q in range(4):
            nc.sync.dma_start(
                out=xs[32 * q : 32 * q + 4 * PASSES, :].bitcast(I32),
                in_=x_scales[:, 4 * q : 4 * q + 4, :].bitcast(I32),
            )
        for i, (g, m0, m1) in enumerate(pieces):
            nc.sync.dma_start(out=w1raw[i][:], in_=rows(w1, g)[:, :, PACK * m0 : PACK * m1])
        nc.sync.dma_start(out=xw[1][:], in_=words(1))
        nc.sync.dma_start(out=w2raw[:], in_=rows(w2, 0))
        for b in range(BLOCKS):
            nc.sync.dma_start(out=window[b][:], in_=res[b * P : (b + 1) * P, :])
        for h in range(2):
            nc.sync.dma_start(out=gate_half[h][:], in_=gate[:, h * S // 2 : (h + 1) * S // 2])

        nc.scalar.activation(warm_out[:], warm_in[:], ACT.Gelu_apprx_tanh)

        xg = [keep.tile([P, S], U32, name="xg0", align_bytes=64)]
        xsg = keep.tile([P, S], U8, name="xsg", align_bytes=64)
        w1g = [keep.tile([P, PACK, P, PACK], BF16, name=f"w1g{g}", align_bytes=64) for g in range(PASSES)]
        w1c = [keep.tile([P, H], U32, name=f"w1c{g}", tag=f"w1c{g}", align_bytes=64) for g in range(PASSES)]
        w1s = [keep.tile([P, H], U8, name=f"w1s{g}", align_bytes=64) for g in range(PASSES)]
        w2s = keep.tile([P, N], U8, name="w2s", align_bytes=64)
        terms = keep.tile([P, 11, CHUNK], F32, name="terms", align_bytes=64)

        def slots(s0, s1):
            return terms[:, s0:s1].rearrange("p s n -> p (s n)")

        total = keep.tile([P, S], F32, name="total", align_bytes=64)

        def deal_w1(g):
            source = w1raw[g][:].rearrange("p j (m t) -> p m j t", t=PACK)
            for engine_copy, t0 in ((nc.vector.tensor_copy, 2), (nc.scalar.copy, 0)):
                engine_copy(w1g[g][:, t0 : t0 + 2].rearrange("p t m j -> p m j t"), source[:, :, :, t0 : t0 + 2])

        def quantise_w1(g, t0):
            cols = slice(t0 * P, (t0 + 2) * P)
            nc.vector.quantize_mx(
                out=w1c[g][:, cols].bitcast(FP8X4), scales=w1s[g][:, cols], in_=w1g[g][:, t0 : t0 + 2].rearrange("p t m j -> p (t m j)")
            )

        acc = [psum.tile([P, PACK, CHUNK], F32, name=f"hid{c}", tag=f"hid{c}") for c in range(CHUNKS)]

        def first_product(c, g):
            ent = slice(c * CHUNK, (c + 1) * CHUNK)
            for t in reversed(range(PACK)):
                cols = slice(t * P, (t + 1) * P)
                nc.tensor.matmul_mx(
                    out=acc[c][:, t, :],
                    lhsT=w1c[g][:, cols].bitcast(FP8X4),
                    lhsT_scale=w1s[g][:, cols],
                    rhs=xg[g][:, ent].bitcast(FP8X4),
                    rhs_scale=xsg[4 * g : P, ent],
                    start=(g == 0 and t == PACK - 1),
                    stop=(g == PASSES - 1 and t == 0),
                )

        nc.vector.tensor_copy(xg[0][:], xw[0][:].bitcast(U32).indirect(offsets[:]))
        nc.vector.tensor_copy(xsg[:], xs[:].indirect(offsets[:]))

        xg.append(keep.tile([P, S], U32, name="xg1", align_bytes=64))

        def gather_second_pass(c0, c1):
            lists = offsets[:, c0 * CHUNK // LANES : c1 * CHUNK // LANES]
            nc.vector.tensor_copy(xg[1][:, c0 * CHUNK : c1 * CHUNK], xw[1][:].bitcast(U32).indirect(lists))

        deal_w1(0)
        quantise_w1(0, 2)
        quantise_w1(0, 0)
        first_product(0, 0)
        first_product(1, 0)
        deal_w1(1)
        quantise_w1(1, 2)
        gather_second_pass(0, 1)
        quantise_w1(1, 0)
        gather_second_pass(1, 2)
        gather_second_pass(2, 4)

        def lists(c0, c1):
            return offsets[:, c0 * CHUNK // LANES : c1 * CHUNK // LANES]

        def span(c0, c1):
            return slice(c0 * CHUNK, c1 * CHUNK)

        w2g = keep.tile([P, N, PACK], BF16, name="w2g", tag="w2g", align_bytes=64)
        nc.vector.tensor_copy(
            w2g[:].rearrange("p (c i) j -> p c j i", i=4),
            w2raw[:].rearrange("p j (c i) -> p c j i", i=4),
        )

        hg = keep.tile([P, CHUNKS, CHUNK, PACK], BF16, name="hg", align_bytes=64)
        hc = [keep.tile([P, S // 2], U32, name="hc0", align_bytes=64)]
        hs = keep.tile([P, S], U8, name="hs", align_bytes=64)
        w2c = keep.tile([P, N], U32, name="w2c", align_bytes=64)

        def hidden(c):
            first_product(c, 1)
            nc.scalar.activation(hg[:, c], acc[c][:].rearrange("p t n -> p n t"), ACT.Gelu_apprx_tanh)

        def quantise_hidden(c0, c1):
            nc.vector.quantize_mx(
                out=hc[c0 // 2][:, span(c0 % 2, c0 % 2 + c1 - c0)].bitcast(FP8X4), scales=hs[:, span(c0, c1)], in_=hg[:, c0:c1].rearrange("p c n t -> p (c n t)")
            )

        def second(y, b, c0, c1):
            cols = slice(b * P, (b + 1) * P)
            nc.tensor.matmul_mx(
                out=y,
                lhsT=w2c[:, cols].bitcast(FP8X4),
                lhsT_scale=w2s[:, cols],
                rhs=hc[c0 // 2][:].bitcast(FP8X4),
                rhs_scale=hs[:, span(c0, c1)],
                start=True,
                stop=True,
            )

        def put_scalar(c0, c1):
            nc.scalar.activation(window[0][:].indirect(lists(c0, c1)), total[:, span(c0, c1)], ACT.Copy)

        def gated(values, y, c0, c1):
            nc.vector.tensor_tensor(values, y, gate_half[c0 // 2][:], MULT)

        def add(values, h):
            nc.vector.tensor_tensor(total[:, span(2 * h, 2 * h + 2)], values, slots(3 + 2 * h, 5 + 2 * h), ADD)

        y_a = [psum.tile([P, 2 * CHUNK], F32, name=f"y_a{h}", tag=f"y_a{h}") for h in range(2)]
        y_b = [psum.tile([P, 2 * CHUNK], F32, name=f"y_b{h}", tag=f"y_b{h}") for h in range(2)]
        gated_a = keep.tile([P, S], F32, name="gated_a", align_bytes=64)

        hidden(0)
        first_product(2, 0)
        hidden(1)
        first_product(3, 0)
        quantise_hidden(0, 1)
        nc.vector.quantize_mx(out=w2c[:].bitcast(FP8X4), scales=w2s[:], in_=w2g[:].rearrange("p n j -> p (n j)"))
        hidden(2)
        quantise_hidden(1, 2)
        second(y_a[0][:], 0, 0, 2)
        second(y_b[0][:], 1, 0, 2)
        hidden(3)
        nc.vector.tensor_copy(slots(3, 5), window[0][:].indirect(lists(0, 2)))
        nc.scalar.activation(slots(5, 7), window[0][:].indirect(lists(2, 4)), ACT.Copy)
        nc.scalar.activation(slots(7, 10), window[1][:].indirect(lists(0, 3)), ACT.Copy)
        gated(gated_a[:, span(0, 2)], y_a[0][:], 0, 2)
        gated(slots(0, 2), y_b[0][:], 0, 2)
        add(gated_a[:, span(0, 2)], 0)
        hc.append(keep.tile([P, S // 2], U32, name="hc1", tag="gate_half0", align_bytes=64))
        quantise_hidden(2, 4)
        second(y_a[1][:], 0, 2, 4)
        second(y_b[1][:], 1, 2, 4)
        nc.vector.tensor_copy(slots(3, 4), window[1][:].indirect(lists(3, 4)))
        gated(gated_a[:, span(2, 4)], y_a[1][:], 2, 4)
        nc.vector.tensor_tensor(
            terms[:, 2:11:8], y_b[1][:].rearrange("p (c n) -> p c n", c=2), gate_half[1][:].rearrange("p (c n) -> p c n", c=2), MULT
        )
        add(gated_a[:, span(2, 4)], 1)
        put_scalar(0, 2)
        put_scalar(2, 4)
        nc.vector.tensor_tensor(window[1][:].indirect(offsets[:]), slots(0, 4), slots(7, 11), ADD)
        nc.sync.dma_start(out=out[0:P, :], in_=window[0][:])
        nc.sync.dma_start(out=out[P : 2 * P, :], in_=window[1][:])
